import numpy as np
import ml_dtypes


def mxq(x, axis, fmt="e4m3"):
    dtype, down = {"e4m3": (ml_dtypes.float8_e4m3fn, 7), "e5m2": (ml_dtypes.float8_e5m2, 14)}[fmt]
    v = np.moveaxis(np.asarray(x, np.float32).astype(ml_dtypes.bfloat16).astype(np.float64), axis, -1)
    blocks = v.reshape(v.shape[:-1] + (-1, 32))
    amax = np.abs(blocks).max(-1, keepdims=True)
    byte = np.maximum(np.where(amax > 0, np.frexp(amax)[1] - 1 + 127, 0) - down, 1)
    scale = np.exp2(byte - 127.0)
    codes = (blocks / scale).astype(np.float32).astype(dtype).astype(np.float64)
    return np.moveaxis((codes * scale).reshape(v.shape), -1, axis)


WIDE = False


def mx_kscale(k):
    if not WIDE:
        return np.ones(k)
    levels = np.array([24, -24, 12, -12, 0])
    if k % 512:
        return np.exp2(np.random.permutation(np.resize(levels, k // 32))).repeat(32)
    a = np.empty((k // 512, 16))
    for p in range(k // 512):
        a[p, :8] = np.random.permutation(np.resize(levels, 8))
        for g in range(8):
            far = levels[np.abs(levels - a[p, g]) >= 10]
            a[p, g + 8] = far[np.random.randint(len(far))]
    return np.exp2(a.ravel()).repeat(32)


def f64(x):
    return np.asarray(x).astype(np.float64)


def striped8(idx):
    return np.concatenate([v.reshape(-1, 16).T for v in idx]).astype(np.uint16)


def unstriped8(offs):
    return np.stack([offs[16 * g:16 * g + 16].T.reshape(-1) for g in range(8)]).astype(np.int64)


E2M1 = np.array([0.0, 0.5, 1.0, 1.5, 2.0, 3.0, 4.0, 6.0, -0.0, -0.5, -1.0, -1.5, -2.0, -3.0, -4.0, -6.0])


def pack_weight(w, fmt):
    k, n = w.shape
    w = f64(np.asarray(w, np.float32).astype(ml_dtypes.bfloat16)).reshape(k // 32, 32, n)
    amax = np.abs(w).max(1)
    if fmt == "e4m3":
        byte = np.frexp(amax)[1] - 1 + 127 - 7
    else:
        mant, ex = np.frexp(amax / 6.0)
        byte = np.where(mant > 0.5, ex, ex - 1) + 127
    byte = np.clip(np.where(amax > 0, byte, 1), 1, 254)
    scaled = (w * np.exp2(127.0 - byte)[:, None, :]).reshape(k, n).astype(np.float32)
    by_word = np.ascontiguousarray(scaled.reshape(k // 512, 128, 4, n).transpose(0, 1, 3, 2))
    if fmt == "e4m3":
        words = by_word.astype(ml_dtypes.float8_e4m3fn).view(np.uint8)
    else:
        c = by_word.astype(ml_dtypes.float4_e2m1fn).view(np.uint8) & 0xF
        words = (c[..., 0::2] | (c[..., 1::2] << 4)).reshape(k // 512, 128, 2 * n)
    return np.ascontiguousarray(words), np.ascontiguousarray(byte.astype(np.uint8).reshape(k // 512, 16, n))


def unpack_weight(words, scales, fmt):
    g, _, n = scales.shape
    words = np.ascontiguousarray(words).reshape(g, 128, n, -1)
    if fmt == "e4m3":
        vals = words.view(ml_dtypes.float8_e4m3fn).astype(np.float64)
    else:
        nib = np.empty((g, 128, n, 4), np.uint8)
        nib[..., 0::2] = words & 0xF
        nib[..., 1::2] = words >> 4
        vals = E2M1[nib]
    vals = vals * np.repeat(np.exp2(scales.astype(np.float64) - 127.0), 8, axis=1)[..., None]
    return vals.transpose(0, 1, 3, 2).reshape(g * 512, n)


def planes(y):
    n, m = y.shape
    v = y.astype(np.float32).astype(ml_dtypes.bfloat16).astype(np.float64).reshape(n // 32, 32, m)
    top = np.abs(v).max(1)
    byte = np.clip(np.where(top > 0, np.frexp(top)[1] - 1 + 127 - 7, 1), 1, 254)
    codes = (v * np.exp2(127.0 - byte)[:, None, :]).reshape(n, m).astype(np.float32).astype(ml_dtypes.float8_e4m3fn).view(np.uint8)
    words = codes.reshape(n // 512, 128, 4, m).transpose(0, 1, 3, 2)
    return np.ascontiguousarray(words), np.ascontiguousarray(byte.astype(np.uint8).reshape(n // 512, 16, m))


def sigm(f):
    return 1.0 / (1.0 + np.exp(-np.maximum(f, -700.0)))


K, N, T, J = 512, 512, 2048, 1024


def setup_inputs():
    n = np.random.standard_normal
    s = mx_kscale(K)[:, None]
    p_wk = pack_weight(n((K, N)) / np.sqrt(K) / s, "e2m1")
    p_wv = pack_weight(n((K, N)) / np.sqrt(K) / s, "e4m3")
    return {
        "xT": (n((K, T)) * s).astype(np.float32),
        "wgt": np.repeat(np.random.uniform(0.5, 2.0, (8, J)), 16, axis=0).astype(np.float32),
        "wk_words": p_wk[0],
        "wk_scales": p_wk[1],
        "wv_words": p_wv[0],
        "wv_scales": p_wv[1],
        "bg": (0.3 * n(N) - 1.0).astype(np.float32),
        "res": (n((N, J))).astype(np.float32),
        "offs": striped8(np.stack([np.random.permutation(T)[:J] for _ in range(8)])),
    }


def reference(xT, wgt, wk_words, wk_scales, wv_words, wv_scales, bg, res, offs):
    idx = unstriped8(offs)
    rows = np.arange(K)
    xg = f64(wgt)[rows // 4 % 128] * f64(xT)[rows[:, None], idx[rows % 512 // 64]]
    xT_ = mxq(xg, 0, "e4m3")
    wk_ = unpack_weight(wk_words, wk_scales, "e2m1")
    wv_ = unpack_weight(wv_words, wv_scales, "e4m3")
    ke = wk_.T @ xT_
    ve = wv_.T @ xT_
    gate = sigm(ke + f64(bg)[:, None])
    out_0 = f64(res) + gate * (np.tanh(ve) - f64(res))
    return (out_0,) + planes(out_0)

@@ -1,0 +1,171 @@
+from contextlib import ExitStack
+
+import concourse.mybir as mybir
+
+K, N, T, J = 512, 512, 2048, 1024
+FLOPS = 2 * 2 * K * N * J
+
+F32 = mybir.dt.float32
+BF16 = mybir.dt.bfloat16
+I32 = mybir.dt.int32
+U16 = mybir.dt.uint16
+U8 = mybir.dt.uint8
+FP8X4 = mybir.dt.float8_e4m3fn_x4
+FP4X4 = mybir.dt.float4_e2m1fn_x4
+ALU = mybir.AluOpType
+ACT = mybir.ActivationFunctionType
+
+P = 128
+PACK = 4
+GROUP = 16
+BANK = 512
+WIDTHS = [128, 256, 256, 256, 128]
+HALF = J // 2
+
+
+def tile_list_hwaytanhP_kernel(
+    tc, xT, wgt, wk_words, wk_scales, wv_words, wv_scales, bg, res, offs, out_0, out_1, out_2
+):
+    nc = tc.nc
+    starts = [sum(WIDTHS[:c]) for c in range(len(WIDTHS))]
+    chunks = len(WIDTHS)
+
+    x_planes = xT.rearrange("(p i) t -> p i t", i=PACK)
+    res_rows = res.rearrange("(p i) j -> p i j", i=PACK)
+    out_rows = out_0.rearrange("(p i) j -> p i j", i=PACK)
+    out_words = out_1[0].rearrange("p j i -> p (j i)").bitcast(I32)
+
+    with ExitStack() as ctx:
+        keep = ctx.enter_context(tc.tile_pool(name="keep", bufs=1))
+        psum = ctx.enter_context(tc.psum_pool(name="psum", bufs=2))
+
+        offsets = keep.tile([P, J // GROUP], U16, name="offsets")
+        wk_raw = keep.tile([P, 2 * N], U8, name="wk_raw", align_bytes=64)
+        wv_raw = keep.tile([P, N], I32, name="wv_raw", align_bytes=64)
+        sk_raw = keep.tile([P, N], U8, name="sk_raw", align_bytes=64)
+        sv_raw = keep.tile([P, N], U8, name="sv_raw", align_bytes=64)
+        wk = keep.tile([P, PACK, 2 * P], U8, name="wk", align_bytes=64)
+        wv = keep.tile([P, PACK, P], I32, name="wv", align_bytes=64)
+        sk = keep.tile([P, PACK, P], U8, name="sk", align_bytes=64)
+        sv = keep.tile([P, PACK, P], U8, name="sv", align_bytes=64)
+        bias = keep.tile([P, PACK], F32, name="bias")
+        warm = keep.tile([P, 8], F32, name="warm")
+        warm_out = keep.tile([P, 8], F32, name="warm_out")
+        planes = [keep.tile([P, T], F32, name="plane%d" % i) for i in range(PACK)]
+        wgt_sb = keep.tile([P, J], F32, name="wgt_sb")
+        res_sb = keep.tile([P, PACK, J], F32, name="res_sb")
+        y_scales = keep.tile([P, J], U8, name="y_scales", align_bytes=64)
+
+        nc.vector.memset(sk_raw[:].bitcast(I32), 0)
+        nc.vector.memset(sv_raw[:].bitcast(I32), 0)
+        nc.vector.memset(warm[:], 0.0)
+        nc.scalar.activation(warm_out[:], warm[:], ACT.Sigmoid)
+
+        nc.sync.dma_start(wk_raw[:].bitcast(I32), wk_words[0].bitcast(I32))
+        nc.sync.dma_start(wv_raw[:], wv_words[0].rearrange("p n i -> p (n i)").bitcast(I32))
+        def load_scales(tile, rows):
+            for q in range(4):
+                nc.sync.dma_start(tile[32 * q : 32 * q + 4, :].bitcast(I32), rows[4 * q : 4 * q + 4, :].bitcast(I32))
+
+        load_scales(sk_raw, wk_scales[0])
+        nc.sync.dma_start(offsets[:], offs)
+        nc.sync.dma_start(planes[0][:], x_planes[:, 0, :])
+        nc.sync.dma_start(wgt_sb[:, :HALF], wgt[:, :HALF])
+        load_scales(sv_raw, wv_scales[0])
+        nc.sync.dma_start(wgt_sb[:, HALF:], wgt[:, HALF:])
+        for i in range(1, PACK):
+            nc.sync.dma_start(planes[i][:], x_planes[:, i, :])
+        nc.sync.dma_start(bias[:], bg.rearrange("(p i) -> p i", i=PACK))
+        nc.sync.dma_start(res_sb[:, :, :HALF], res_rows[:, :, :HALF])
+        nc.sync.dma_start(res_sb[:, :, HALF:], res_rows[:, :, HALF:])
+
+        nc.vector.tensor_copy(
+            wk[:].rearrange("p i (m b) -> p i m b", b=2), wk_raw[:].rearrange("p (m i b) -> p i m b", i=PACK, b=2)
+        )
+        nc.vector.tensor_copy(wv[:], wv_raw[:].rearrange("p (m i) -> p i m", i=PACK))
+        nc.vector.tensor_copy(sk[:], sk_raw[:].rearrange("p (m i) -> p i m", i=PACK))
+
+        picked = [keep.tile([P, PACK, w], F32, name="picked%d" % c) for c, w in enumerate(WIDTHS)]
+        x_bf = [keep.tile([P, PACK * w], BF16, name="x_bf%d" % c, align_bytes=64) for c, w in enumerate(WIDTHS)]
+        x_codes = [keep.tile([P, w], I32, name="x_codes%d" % c, align_bytes=64) for c, w in enumerate(WIDTHS)]
+        x_scales = [keep.tile([P, w], U8, name="x_scales%d" % c, align_bytes=64) for c, w in enumerate(WIDTHS)]
+        cand = [keep.tile([P, PACK, w], F32, name="cand%d" % c) for c, w in enumerate(WIDTHS)]
+        gate = [keep.tile([P, PACK, w], F32, name="gate%d" % c) for c, w in enumerate(WIDTHS)]
+        diff = [keep.tile([P, PACK, w], F32, name="diff%d" % c) for c, w in enumerate(WIDTHS)]
+        step = [keep.tile([P, PACK, w], F32, name="step%d" % c) for c, w in enumerate(WIDTHS)]
+        y = [keep.tile([P, PACK, w], F32, name="y%d" % c) for c, w in enumerate(WIDTHS)]
+        y_bf = [keep.tile([P, PACK * w], BF16, name="y_bf%d" % c, align_bytes=64) for c, w in enumerate(WIDTHS)]
+        y_codes = [keep.tile([P, w], I32, name="y_codes%d" % c, align_bytes=64) for c, w in enumerate(WIDTHS)]
+
+        def cols(c):
+            return slice(starts[c], starts[c] + WIDTHS[c])
+
+        def gather(i, c):
+            entries = offsets[:, starts[c] // GROUP : (starts[c] + WIDTHS[c]) // GROUP]
+            nc.vector.tensor_tensor(picked[c][:, i, :], planes[i][:].indirect(entries), wgt_sb[:, cols(c)], ALU.mult)
+
+        def interleave(dst, src, on_vector):
+            dst_view = dst[:].rearrange("p (u e i) -> p u i e", e=2, i=PACK)
+            src_view = src[:].rearrange("p i (u e) -> p u i e", e=2)
+            if on_vector:
+                nc.vector.tensor_copy(dst_view, src_view)
+            else:
+                nc.scalar.copy(dst_view, src_view)
+
+        def products(c):
+            w = WIDTHS[c]
+            per_bank = BANK // w
+            nc.vector.quantize_mx(x_codes[c][:].bitcast(FP8X4), x_scales[c][:], x_bf[c][:])
+            for i0 in range(0, PACK, per_bank):
+                ve = psum.tile([P, per_bank, w], F32, name="ve")
+                for i in range(i0, i0 + per_bank):
+                    nc.tensor.matmul_mx(
+                        ve[:, i - i0, :], wv[:, i, :].bitcast(FP8X4), sv[:, i, :],
+                        x_codes[c][:].bitcast(FP8X4), x_scales[c][:], start=True, stop=True,
+                    )
+                nc.scalar.activation(cand[c][:, i0 : i0 + per_bank, :], ve[:], ACT.Tanh)
+            for i0 in range(0, PACK, per_bank):
+                ke = psum.tile([P, per_bank, w], F32, name="ke")
+                for i in range(i0, i0 + per_bank):
+                    nc.tensor.matmul_mx(
+                        ke[:, i - i0, :], wk[:, i, :].bitcast(FP4X4), sk[:, i, :],
+                        x_codes[c][:].bitcast(FP8X4), x_scales[c][:], start=True, stop=True,
+                    )
+                for i in range(i0, i0 + per_bank):
+                    nc.scalar.activation(gate[c][:, i, :], ke[:, i - i0, :], ACT.Sigmoid, bias=bias[:, i : i + 1])
+
+        def blend(c):
+            halves = [slice(0, 2), slice(2, 4)]
+            for h in halves:
+                nc.vector.tensor_tensor(diff[c][:, h, :], cand[c][:, h, :], res_sb[:, h, cols(c)], ALU.subtract)
+            for h in halves:
+                nc.vector.tensor_tensor(step[c][:, h, :], diff[c][:, h, :], gate[c][:, h, :], ALU.mult)
+            for h in halves:
+                nc.vector.tensor_tensor(y[c][:, h, :], step[c][:, h, :], res_sb[:, h, cols(c)], ALU.add)
+            nc.sync.dma_start(out_rows[:, :, cols(c)], y[c][:])
+            interleave(y_bf[c], y[c], c == chunks - 1)
+
+        def hand_on(c):
+            nc.vector.quantize_mx(y_codes[c][:].bitcast(FP8X4), y_scales[:, cols(c)], y_bf[c][:])
+            nc.sync.dma_start(out_words[:, cols(c)], y_codes[c][:])
+
+        for i in range(PACK - 1):
+            for c in range(chunks):
+                gather(i, c)
+            if i == 0:
+                nc.vector.tensor_copy(sv[:], sv_raw[:].rearrange("p (m i) -> p i m", i=PACK))
+        for s in range(chunks + 3):
+            if s < chunks:
+                gather(PACK - 1, s)
+                interleave(x_bf[s], picked[s], s == 0)
+            if 0 <= s - 1 < chunks:
+                products(s - 1)
+            if 0 <= s - 2 < chunks:
+                blend(s - 2)
+            if 0 <= s - 3 < chunks:
+                hand_on(s - 3)
+        for q in range(4):
+            queue = nc.sync if q % 2 == 0 else nc.scalar
+            queue.dma_start(
+                out_2[0][4 * q : 4 * q + 4, :].bitcast(I32), y_scales[32 * q : 32 * q + 4, :].bitcast(I32)
+            )

@@ -1,6 +1,7 @@
 from contextlib import ExitStack
 
 import concourse.mybir as mybir
+from concourse.masks import make_identity
 
 K, N, T, J = 512, 512, 2048, 1024
 FLOPS = 2 * 2 * K * N * J
@@ -21,6 +22,7 @@ GROUP = 16
 BANK = 512
 WIDTHS = [128, 256, 256, 256, 128]
 HALF = J // 2
+HEADS = 8
 
 
 def tile_list_hwaytanhP_kernel(
@@ -56,36 +58,55 @@ def tile_list_hwaytanhP_kernel(
         res_sb = keep.tile([P, PACK, J], F32, name="res_sb")
         y_scales = keep.tile([P, J], U8, name="y_scales", align_bytes=64)
 
-        nc.vector.memset(sk_raw[:].bitcast(I32), 0)
-        nc.vector.memset(sv_raw[:].bitcast(I32), 0)
+        wgt_rows = keep.tile([P, P], F32, name="wgt_rows")
+        wgt_wide = [keep.tile([P, PACK, P], F32, name="wgt_wide%d" % h) for h in range(2)]
+        ident = keep.tile([P, P], F32, name="ident")
+
+        nc.gpsimd.memset(sk_raw[:].bitcast(I32), 0)
+        nc.gpsimd.memset(sv_raw[:].bitcast(I32), 0)
         nc.vector.memset(warm[:], 0.0)
+        make_identity(nc, ident[:])
         nc.scalar.activation(warm_out[:], warm[:], ACT.Sigmoid)
 
-        nc.sync.dma_start(wk_raw[:].bitcast(I32), wk_words[0].bitcast(I32))
-        nc.sync.dma_start(wv_raw[:], wv_words[0].rearrange("p n i -> p (n i)").bitcast(I32))
         def load_scales(tile, rows):
             for q in range(4):
                 nc.sync.dma_start(tile[32 * q : 32 * q + 4, :].bitcast(I32), rows[4 * q : 4 * q + 4, :].bitcast(I32))
 
+        two_rows = wgt.rearrange("(g r) j -> g (r j)", r=GROUP)[:, : 2 * J]
+        nc.sync.dma_start(wgt_rows[:], two_rows.rearrange("g (s j) -> g s j", j=P))
+        nc.sync.dma_start(wk_raw[:].bitcast(I32), wk_words[0].bitcast(I32))
         load_scales(sk_raw, wk_scales[0])
         nc.sync.dma_start(offsets[:], offs)
         nc.sync.dma_start(planes[0][:], x_planes[:, 0, :])
-        nc.sync.dma_start(wgt_sb[:, :HALF], wgt[:, :HALF])
+        nc.sync.dma_start(planes[1][:], x_planes[:, 1, :])
+        nc.sync.dma_start(wv_raw[:], wv_words[0].rearrange("p n i -> p (n i)").bitcast(I32))
         load_scales(sv_raw, wv_scales[0])
-        nc.sync.dma_start(wgt_sb[:, HALF:], wgt[:, HALF:])
-        for i in range(1, PACK):
+        for i in range(2, PACK):
             nc.sync.dma_start(planes[i][:], x_planes[:, i, :])
         nc.sync.dma_start(bias[:], bg.rearrange("(p i) -> p i", i=PACK))
         nc.sync.dma_start(res_sb[:, :, :HALF], res_rows[:, :, :HALF])
         nc.sync.dma_start(res_sb[:, :, HALF:], res_rows[:, :, HALF:])
 
+        turned = psum.tile([P, HEADS, GROUP], F32, name="ke")
+        nc.tensor.transpose(turned[:].rearrange("j g s -> j (g s)"), wgt_rows[:], ident[:])
+        for h in range(2):
+            heads = turned[:, :, PACK * h : PACK * (h + 1)].rearrange("j g s -> j s g")
+            nc.scalar.copy(
+                wgt_wide[h][:].rearrange("j s (g r) -> j s g r", r=GROUP),
+                heads.unsqueeze(3).to_broadcast([P, PACK, HEADS, GROUP]),
+            )
+        for h in range(2):
+            spread = psum.tile([P, PACK, P], F32, name="ve")
+            for s in range(PACK):
+                nc.tensor.transpose(spread[:, s, :], wgt_wide[h][:, s, :], ident[:])
+            nc.scalar.copy(wgt_sb[:, HALF * h : HALF * (h + 1)], spread[:].rearrange("p s j -> p (s j)"))
+
         nc.vector.tensor_copy(
             wk[:].rearrange("p i (m b) -> p i m b", b=2), wk_raw[:].rearrange("p (m i b) -> p i m b", i=PACK, b=2)
         )
-        nc.vector.tensor_copy(wv[:], wv_raw[:].rearrange("p (m i) -> p i m", i=PACK))
         nc.vector.tensor_copy(sk[:], sk_raw[:].rearrange("p (m i) -> p i m", i=PACK))
 
-        picked = [keep.tile([P, PACK, w], F32, name="picked%d" % c) for c, w in enumerate(WIDTHS)]
+        picked = keep.tile([P, PACK, J], F32, name="picked")
         x_bf = [keep.tile([P, PACK * w], BF16, name="x_bf%d" % c, align_bytes=64) for c, w in enumerate(WIDTHS)]
         x_codes = [keep.tile([P, w], I32, name="x_codes%d" % c, align_bytes=64) for c, w in enumerate(WIDTHS)]
         x_scales = [keep.tile([P, w], U8, name="x_scales%d" % c, align_bytes=64) for c, w in enumerate(WIDTHS)]
@@ -100,13 +121,13 @@ def tile_list_hwaytanhP_kernel(
         def cols(c):
             return slice(starts[c], starts[c] + WIDTHS[c])
 
-        def gather(i, c):
-            entries = offsets[:, starts[c] // GROUP : (starts[c] + WIDTHS[c]) // GROUP]
-            nc.vector.tensor_tensor(picked[c][:, i, :], planes[i][:].indirect(entries), wgt_sb[:, cols(c)], ALU.mult)
+        def gather(i, j0, j1):
+            entries = offsets[:, j0 // GROUP : j1 // GROUP]
+            nc.vector.tensor_tensor(picked[:, i, j0:j1], planes[i][:].indirect(entries), wgt_sb[:, j0:j1], ALU.mult)
 
-        def interleave(dst, src, on_vector):
-            dst_view = dst[:].rearrange("p (u e i) -> p u i e", e=2, i=PACK)
-            src_view = src[:].rearrange("p i (u e) -> p u i e", e=2)
+        def interleave(dst, src, rows, on_vector):
+            dst_view = dst[:].rearrange("p (u e i) -> p u i e", e=2, i=PACK)[:, :, rows, :]
+            src_view = src.rearrange("p i (u e) -> p u i e", e=2)[:, :, rows, :]
             if on_vector:
                 nc.vector.tensor_copy(dst_view, src_view)
             else:
@@ -143,21 +164,24 @@ def tile_list_hwaytanhP_kernel(
             for h in halves:
                 nc.vector.tensor_tensor(y[c][:, h, :], step[c][:, h, :], res_sb[:, h, cols(c)], ALU.add)
             nc.sync.dma_start(out_rows[:, :, cols(c)], y[c][:])
-            interleave(y_bf[c], y[c], c == chunks - 1)
+            interleave(y_bf[c], y[c][:], slice(0, PACK), c == chunks - 1)
 
         def hand_on(c):
             nc.vector.quantize_mx(y_codes[c][:].bitcast(FP8X4), y_scales[:, cols(c)], y_bf[c][:])
             nc.sync.dma_start(out_words[:, cols(c)], y_codes[c][:])
 
-        for i in range(PACK - 1):
-            for c in range(chunks):
-                gather(i, c)
-            if i == 0:
-                nc.vector.tensor_copy(sv[:], sv_raw[:].rearrange("p (m i) -> p i m", i=PACK))
+        for i in range(2):
+            gather(i, 0, HALF)
+            gather(i, HALF, J)
+        for c in range(chunks):
+            interleave(x_bf[c], picked[:, :, cols(c)], slice(0, 2), False)
+        nc.vector.tensor_copy(wv[:], wv_raw[:].rearrange("p (m i) -> p i m", i=PACK))
+        nc.vector.tensor_copy(sv[:], sv_raw[:].rearrange("p (m i) -> p i m", i=PACK))
+        gather(2, 0, J)
         for s in range(chunks + 3):
             if s < chunks:
-                gather(PACK - 1, s)
-                interleave(x_bf[s], picked[s], s == 0)
+                gather(PACK - 1, starts[s], starts[s] + WIDTHS[s])
+                interleave(x_bf[s], picked[:, :, cols(s)], slice(2, PACK), s == 0)
             if 0 <= s - 1 < chunks:
                 products(s - 1)
             if 0 <= s - 2 < chunks:

@@ -22,6 +22,8 @@ GROUP = 16
 BANK = 512
 WIDTHS = [128, 256, 256, 256, 128]
 HALF = J // 2
+TURNED = (3,)
+Y_ON_VECTOR = (4,)
 HEADS = 8
 
 
@@ -39,6 +41,7 @@ def tile_list_hwaytanhP_kernel(
 
     with ExitStack() as ctx:
         keep = ctx.enter_context(tc.tile_pool(name="keep", bufs=1))
+        ring = ctx.enter_context(tc.tile_pool(name="ring", bufs=2))
         psum = ctx.enter_context(tc.psum_pool(name="psum", bufs=2))
 
         offsets = keep.tile([P, J // GROUP], U16, name="offsets")
@@ -106,38 +109,75 @@ def tile_list_hwaytanhP_kernel(
         )
         nc.vector.tensor_copy(sk[:], sk_raw[:].rearrange("p (m i) -> p i m", i=PACK))
 
-        picked = keep.tile([P, PACK, J], F32, name="picked")
+        early = keep.tile([P, 2, J], F32, name="early")
         x_bf = [keep.tile([P, PACK * w], BF16, name="x_bf%d" % c, align_bytes=64) for c, w in enumerate(WIDTHS)]
         x_codes = [keep.tile([P, w], I32, name="x_codes%d" % c, align_bytes=64) for c, w in enumerate(WIDTHS)]
         x_scales = [keep.tile([P, w], U8, name="x_scales%d" % c, align_bytes=64) for c, w in enumerate(WIDTHS)]
-        cand = [keep.tile([P, PACK, w], F32, name="cand%d" % c) for c, w in enumerate(WIDTHS)]
+        cand = {c: keep.tile([P, PACK, w], F32, name="cand%d" % c) for c, w in enumerate(WIDTHS) if c not in TURNED}
         gate = [keep.tile([P, PACK, w], F32, name="gate%d" % c) for c, w in enumerate(WIDTHS)]
-        diff = [keep.tile([P, PACK, w], F32, name="diff%d" % c) for c, w in enumerate(WIDTHS)]
+        diff = {c: keep.tile([P, PACK, w], F32, name="diff%d" % c) for c, w in enumerate(WIDTHS) if c not in TURNED}
         step = [keep.tile([P, PACK, w], F32, name="step%d" % c) for c, w in enumerate(WIDTHS)]
         y = [keep.tile([P, PACK, w], F32, name="y%d" % c) for c, w in enumerate(WIDTHS)]
         y_bf = [keep.tile([P, PACK * w], BF16, name="y_bf%d" % c, align_bytes=64) for c, w in enumerate(WIDTHS)]
         y_codes = [keep.tile([P, w], I32, name="y_codes%d" % c, align_bytes=64) for c, w in enumerate(WIDTHS)]
 
+        res_t = {c: keep.tile([P, 2, PACK, P], F32, name="res_t%d" % c) for c in TURNED}
+        neg_t = {c: keep.tile([P, 2, PACK, P], F32, name="neg_t%d" % c) for c in TURNED}
+        gap = {}
+
         def cols(c):
             return slice(starts[c], starts[c] + WIDTHS[c])
 
-        def gather(i, j0, j1):
+        def gather(dst, i, j0, j1):
             entries = offsets[:, j0 // GROUP : j1 // GROUP]
-            nc.vector.tensor_tensor(picked[:, i, j0:j1], planes[i][:].indirect(entries), wgt_sb[:, j0:j1], ALU.mult)
+            nc.vector.tensor_tensor(dst, planes[i][:].indirect(entries), wgt_sb[:, j0:j1], ALU.mult)
 
         def interleave(dst, src, rows, on_vector):
             dst_view = dst[:].rearrange("p (u e i) -> p u i e", e=2, i=PACK)[:, :, rows, :]
-            src_view = src.rearrange("p i (u e) -> p u i e", e=2)[:, :, rows, :]
+            src_view = src.rearrange("p i (u e) -> p u i e", e=2)
             if on_vector:
                 nc.vector.tensor_copy(dst_view, src_view)
             else:
                 nc.scalar.copy(dst_view, src_view)
 
+        def turn_res(c):
+            for b in range(2):
+                bank = psum.tile([P, PACK, P], F32, name="rt")
+                j0 = starts[c] + P * b
+                for i in range(PACK):
+                    nc.tensor.transpose(bank[:, i, :], res_sb[:, i, j0 : j0 + P], ident[:])
+                nc.scalar.copy(res_t[c][:, b, :, :], bank[:])
+
+        def turned_candidates(c):
+            for b in range(2):
+                block = slice(P * b, P * (b + 1))
+                ve = psum.tile([P, N], F32, name="ve")
+                nc.tensor.matmul_mx(
+                    ve[:], x_codes[c][:, block].bitcast(FP8X4), x_scales[c][:, block],
+                    wv_raw[:].bitcast(FP8X4), sv_raw[:], start=True, stop=True,
+                )
+                nc.scalar.activation(
+                    neg_t[c][:, b, :, :], ve[:].rearrange("j (m i) -> j i m", i=PACK), ACT.Tanh, scale=-1.0
+                )
+
+        def turned_gap(c):
+            for h in range(2):
+                bank = psum.tile([P, 2, 2 * P], F32, name="gap")
+                terms = [(src, i, b) for src in (res_t[c], neg_t[c]) for b in range(2) for i in range(2)]
+                for n, (src, i, b) in enumerate(terms):
+                    nc.tensor.matmul(
+                        bank[:, i, P * b : P * (b + 1)], src[:, b, 2 * h + i, :], ident[:],
+                        start=(n == 0), stop=(n == len(terms) - 1), is_transpose=True,
+                    )
+                gap[c, h] = bank
+
         def products(c):
             w = WIDTHS[c]
             per_bank = BANK // w
             nc.vector.quantize_mx(x_codes[c][:].bitcast(FP8X4), x_scales[c][:], x_bf[c][:])
-            for i0 in range(0, PACK, per_bank):
+            if c in TURNED:
+                turned_candidates(c)
+            for i0 in range(0, PACK if c not in TURNED else 0, per_bank):
                 ve = psum.tile([P, per_bank, w], F32, name="ve")
                 for i in range(i0, i0 + per_bank):
                     nc.tensor.matmul_mx(
@@ -154,40 +194,50 @@ def tile_list_hwaytanhP_kernel(
                     )
                 for i in range(i0, i0 + per_bank):
                     nc.scalar.activation(gate[c][:, i, :], ke[:, i - i0, :], ACT.Sigmoid, bias=bias[:, i : i + 1])
+            if c in TURNED:
+                turned_gap(c)
 
         def blend(c):
             halves = [slice(0, 2), slice(2, 4)]
-            for h in halves:
-                nc.vector.tensor_tensor(diff[c][:, h, :], cand[c][:, h, :], res_sb[:, h, cols(c)], ALU.subtract)
-            for h in halves:
-                nc.vector.tensor_tensor(step[c][:, h, :], diff[c][:, h, :], gate[c][:, h, :], ALU.mult)
-            for h in halves:
-                nc.vector.tensor_tensor(y[c][:, h, :], step[c][:, h, :], res_sb[:, h, cols(c)], ALU.add)
+            if c in TURNED:
+                for n, h in enumerate(halves):
+                    nc.vector.tensor_tensor(step[c][:, h, :], gap[c, n][:], gate[c][:, h, :], ALU.mult)
+                for h in halves:
+                    nc.vector.tensor_tensor(y[c][:, h, :], res_sb[:, h, cols(c)], step[c][:, h, :], ALU.subtract)
+            else:
+                for h in halves:
+                    nc.vector.tensor_tensor(diff[c][:, h, :], cand[c][:, h, :], res_sb[:, h, cols(c)], ALU.subtract)
+                for h in halves:
+                    nc.vector.tensor_tensor(step[c][:, h, :], diff[c][:, h, :], gate[c][:, h, :], ALU.mult)
+                for h in halves:
+                    nc.vector.tensor_tensor(y[c][:, h, :], step[c][:, h, :], res_sb[:, h, cols(c)], ALU.add)
             nc.sync.dma_start(out_rows[:, :, cols(c)], y[c][:])
-            interleave(y_bf[c], y[c][:], slice(0, PACK), c == chunks - 1)
+            interleave(y_bf[c], y[c][:], slice(0, PACK), c in Y_ON_VECTOR)
 
         def hand_on(c):
             nc.vector.quantize_mx(y_codes[c][:].bitcast(FP8X4), y_scales[:, cols(c)], y_bf[c][:])
             nc.sync.dma_start(out_words[:, cols(c)], y_codes[c][:])
 
         for i in range(2):
-            gather(i, 0, HALF)
-            gather(i, HALF, J)
-        for c in range(chunks):
-            interleave(x_bf[c], picked[:, :, cols(c)], slice(0, 2), False)
+            gather(early[:, i, :HALF], i, 0, HALF)
+            gather(early[:, i, HALF:], i, HALF, J)
         nc.vector.tensor_copy(wv[:], wv_raw[:].rearrange("p (m i) -> p i m", i=PACK))
         nc.vector.tensor_copy(sv[:], sv_raw[:].rearrange("p (m i) -> p i m", i=PACK))
-        gather(2, 0, J)
-        for s in range(chunks + 3):
+        for s in range(chunks + 4):
             if s < chunks:
-                gather(PACK - 1, starts[s], starts[s] + WIDTHS[s])
-                interleave(x_bf[s], picked[:, :, cols(s)], slice(2, PACK), s == 0)
+                interleave(x_bf[s], early[:, :, cols(s)], slice(0, 2), False)
+                late = ring.tile([P, 2, WIDTHS[s]], F32, name="late")
+                for i in range(2, PACK):
+                    gather(late[:, i - 2, :], i, starts[s], starts[s] + WIDTHS[s])
+                interleave(x_bf[s], late[:], slice(2, PACK), s == 0)
             if 0 <= s - 1 < chunks:
                 products(s - 1)
-            if 0 <= s - 2 < chunks:
-                blend(s - 2)
+            if s in TURNED:
+                turn_res(s)
             if 0 <= s - 3 < chunks:
-                hand_on(s - 3)
+                blend(s - 3)
+            if 0 <= s - 4 < chunks:
+                hand_on(s - 4)
         for q in range(4):
             queue = nc.sync if q % 2 == 0 else nc.scalar
             queue.dma_start(

@@ -20,11 +20,17 @@ P = 128
 PACK = 4
 GROUP = 16
 BANK = 512
-WIDTHS = [128, 256, 256, 256, 128]
-HALF = J // 2
-TURNED = (3,)
-Y_ON_VECTOR = (4,)
 HEADS = 8
+HALF = J // 2
+WIDTHS = [128, 256, 256, 256, 128]
+X_ON_VECTOR = ()
+Y_ON_VECTOR = (4,)
+SPREADS = 4
+SPLIT = (0, 1, 2, 3, 4)
+SLOTS = 2
+SLOT = 256
+TURNED = (3,)
+RES_PIECES = 4
 
 
 def tile_list_hwaytanhP_kernel(
@@ -41,7 +47,6 @@ def tile_list_hwaytanhP_kernel(
 
     with ExitStack() as ctx:
         keep = ctx.enter_context(tc.tile_pool(name="keep", bufs=1))
-        ring = ctx.enter_context(tc.tile_pool(name="ring", bufs=2))
         psum = ctx.enter_context(tc.psum_pool(name="psum", bufs=2))
 
         offsets = keep.tile([P, J // GROUP], U16, name="offsets")
@@ -60,62 +65,67 @@ def tile_list_hwaytanhP_kernel(
         wgt_sb = keep.tile([P, J], F32, name="wgt_sb")
         res_sb = keep.tile([P, PACK, J], F32, name="res_sb")
         y_scales = keep.tile([P, J], U8, name="y_scales", align_bytes=64)
-
         wgt_rows = keep.tile([P, P], F32, name="wgt_rows")
-        wgt_wide = [keep.tile([P, PACK, P], F32, name="wgt_wide%d" % h) for h in range(2)]
+        wgt_wide = [keep.tile([P, HEADS // SPREADS, P], F32, name="wgt_wide%d" % h) for h in range(SPREADS)]
         ident = keep.tile([P, P], F32, name="ident")
 
-        nc.gpsimd.memset(sk_raw[:].bitcast(I32), 0)
-        nc.gpsimd.memset(sv_raw[:].bitcast(I32), 0)
+        nc.vector.memset(sk_raw[:].bitcast(I32), 0)
         nc.vector.memset(warm[:], 0.0)
+        nc.vector.memset(wgt_rows[P // 2 :, :], 0.0)
+        nc.vector.memset(sv_raw[:].bitcast(I32), 0)
         make_identity(nc, ident[:])
-        nc.scalar.activation(warm_out[:], warm[:], ACT.Sigmoid)
 
-        def load_scales(tile, rows):
+        def load_scales(queue, tile, rows):
             for q in range(4):
-                nc.sync.dma_start(tile[32 * q : 32 * q + 4, :].bitcast(I32), rows[4 * q : 4 * q + 4, :].bitcast(I32))
+                queue.dma_start(tile[32 * q : 32 * q + 4, :].bitcast(I32), rows[4 * q : 4 * q + 4, :].bitcast(I32))
 
-        two_rows = wgt.rearrange("(g r) j -> g (r j)", r=GROUP)[:, : 2 * J]
-        nc.sync.dma_start(wgt_rows[:], two_rows.rearrange("g (s j) -> g s j", j=P))
+        one_row = wgt.rearrange("(g r) j -> g r j", r=GROUP)[:, 0, :]
+        nc.sync.dma_start(wgt_rows[: P // 2, :], one_row.rearrange("g (s j) -> g s j", j=P))
         nc.sync.dma_start(wk_raw[:].bitcast(I32), wk_words[0].bitcast(I32))
-        load_scales(sk_raw, wk_scales[0])
+        load_scales(nc.sync, sk_raw, wk_scales[0])
         nc.sync.dma_start(offsets[:], offs)
         nc.sync.dma_start(planes[0][:], x_planes[:, 0, :])
         nc.sync.dma_start(planes[1][:], x_planes[:, 1, :])
         nc.sync.dma_start(wv_raw[:], wv_words[0].rearrange("p n i -> p (n i)").bitcast(I32))
-        load_scales(sv_raw, wv_scales[0])
-        for i in range(2, PACK):
-            nc.sync.dma_start(planes[i][:], x_planes[:, i, :])
+        load_scales(nc.sync, sv_raw, wv_scales[0])
+        nc.sync.dma_start(planes[2][:], x_planes[:, 2, :])
+        nc.sync.dma_start(planes[3][:], x_planes[:, 3, :])
         nc.sync.dma_start(bias[:], bg.rearrange("(p i) -> p i", i=PACK))
-        nc.sync.dma_start(res_sb[:, :, :HALF], res_rows[:, :, :HALF])
-        nc.sync.dma_start(res_sb[:, :, HALF:], res_rows[:, :, HALF:])
+        for a in range(RES_PIECES):
+            piece = slice(a * J // RES_PIECES, (a + 1) * J // RES_PIECES)
+            nc.sync.dma_start(res_sb[:, :, piece], res_rows[:, :, piece])
+        nc.scalar.activation(warm_out[:], warm[:], ACT.Sigmoid)
 
-        turned = psum.tile([P, HEADS, GROUP], F32, name="ke")
-        nc.tensor.transpose(turned[:].rearrange("j g s -> j (g s)"), wgt_rows[:], ident[:])
-        for h in range(2):
-            heads = turned[:, :, PACK * h : PACK * (h + 1)].rearrange("j g s -> j s g")
+        turned = psum.tile([P, 2, HEADS, HEADS], F32, name="ke")
+        nc.tensor.transpose(turned[:].rearrange("j z g s -> j (z g s)"), wgt_rows[:], ident[:])
+        for h in range(SPREADS):
+            per = HEADS // SPREADS
+            heads = turned[:, 0, :, per * h : per * (h + 1)].rearrange("j g s -> j s g")
             nc.scalar.copy(
                 wgt_wide[h][:].rearrange("j s (g r) -> j s g r", r=GROUP),
-                heads.unsqueeze(3).to_broadcast([P, PACK, HEADS, GROUP]),
+                heads.unsqueeze(3).to_broadcast([P, per, HEADS, GROUP]),
             )
-        for h in range(2):
-            spread = psum.tile([P, PACK, P], F32, name="ve")
-            for s in range(PACK):
+            spread = psum.tile([P, per, P], F32, name="ve")
+            for s in range(per):
                 nc.tensor.transpose(spread[:, s, :], wgt_wide[h][:, s, :], ident[:])
-            nc.scalar.copy(wgt_sb[:, HALF * h : HALF * (h + 1)], spread[:].rearrange("p s j -> p (s j)"))
+            nc.scalar.copy(wgt_sb[:, per * P * h : per * P * (h + 1)], spread[:].rearrange("p s j -> p (s j)"))
 
-        nc.vector.tensor_copy(
-            wk[:].rearrange("p i (m b) -> p i m b", b=2), wk_raw[:].rearrange("p (m i b) -> p i m b", i=PACK, b=2)
-        )
-        nc.vector.tensor_copy(sk[:], sk_raw[:].rearrange("p (m i) -> p i m", i=PACK))
+        def sort_k():
+            nc.vector.tensor_copy(wk[:].bitcast(U16), wk_raw[:].bitcast(U16).rearrange("p (m i) -> p i m", i=PACK))
+            nc.vector.tensor_copy(sk[:], sk_raw[:].rearrange("p (m i) -> p i m", i=PACK))
+
+        def sort_v():
+            nc.vector.tensor_copy(wv[:], wv_raw[:].rearrange("p (m i) -> p i m", i=PACK))
+            nc.vector.tensor_copy(sv[:], sv_raw[:].rearrange("p (m i) -> p i m", i=PACK))
 
         early = keep.tile([P, 2, J], F32, name="early")
+        late = keep.tile([P, 2 * (J + SLOTS * SLOT)], F32, name="late")
         x_bf = [keep.tile([P, PACK * w], BF16, name="x_bf%d" % c, align_bytes=64) for c, w in enumerate(WIDTHS)]
         x_codes = [keep.tile([P, w], I32, name="x_codes%d" % c, align_bytes=64) for c, w in enumerate(WIDTHS)]
         x_scales = [keep.tile([P, w], U8, name="x_scales%d" % c, align_bytes=64) for c, w in enumerate(WIDTHS)]
-        cand = {c: keep.tile([P, PACK, w], F32, name="cand%d" % c) for c, w in enumerate(WIDTHS) if c not in TURNED}
+        cand = [keep.tile([P, PACK, w], F32, name="cand%d" % c) for c, w in enumerate(WIDTHS)]
         gate = [keep.tile([P, PACK, w], F32, name="gate%d" % c) for c, w in enumerate(WIDTHS)]
-        diff = {c: keep.tile([P, PACK, w], F32, name="diff%d" % c) for c, w in enumerate(WIDTHS) if c not in TURNED}
+        diff = [keep.tile([P, PACK, w], F32, name="diff%d" % c) for c, w in enumerate(WIDTHS)]
         step = [keep.tile([P, PACK, w], F32, name="step%d" % c) for c, w in enumerate(WIDTHS)]
         y = [keep.tile([P, PACK, w], F32, name="y%d" % c) for c, w in enumerate(WIDTHS)]
         y_bf = [keep.tile([P, PACK * w], BF16, name="y_bf%d" % c, align_bytes=64) for c, w in enumerate(WIDTHS)]
@@ -124,6 +134,25 @@ def tile_list_hwaytanhP_kernel(
         res_t = {c: keep.tile([P, 2, PACK, P], F32, name="res_t%d" % c) for c in TURNED}
         neg_t = {c: keep.tile([P, 2, PACK, P], F32, name="neg_t%d" % c) for c in TURNED}
         gap = {}
+
+        def turn_res(c):
+            for b in range(2):
+                bank = psum.tile([P, PACK, P], F32, name="rt")
+                j0 = starts[c] + P * b
+                for i in range(PACK):
+                    nc.tensor.transpose(bank[:, i, :], res_sb[:, i, j0 : j0 + P], ident[:])
+                nc.scalar.copy(res_t[c][:, b, :, :], bank[:])
+
+        def turned_gap(c):
+            for h in range(2):
+                bank = psum.tile([P, 2, 2 * P], F32, name="gap")
+                terms = [(src, i, b) for src in (res_t[c], neg_t[c]) for b in range(2) for i in range(2)]
+                for n, (src, i, b) in enumerate(terms):
+                    nc.tensor.matmul(
+                        bank[:, i, P * b : P * (b + 1)], src[:, b, 2 * h + i, :], ident[:],
+                        start=(n == 0), stop=(n == len(terms) - 1), is_transpose=True,
+                    )
+                gap[c, h] = bank
 
         def cols(c):
             return slice(starts[c], starts[c] + WIDTHS[c])
@@ -140,52 +169,39 @@ def tile_list_hwaytanhP_kernel(
             else:
                 nc.scalar.copy(dst_view, src_view)
 
-        def turn_res(c):
-            for b in range(2):
-                bank = psum.tile([P, PACK, P], F32, name="rt")
-                j0 = starts[c] + P * b
-                for i in range(PACK):
-                    nc.tensor.transpose(bank[:, i, :], res_sb[:, i, j0 : j0 + P], ident[:])
-                nc.scalar.copy(res_t[c][:, b, :, :], bank[:])
+        def front(c):
+            w = WIDTHS[c]
+            slot = J + SLOT * (c % SLOTS)
+            gather(late[:, slot : slot + w], 3, starts[c], starts[c] + w)
+            pair = late[:, starts[c] : 2 * slot - starts[c]].rearrange("p (r x) -> p r x", r=2)[:, :, :w]
+            interleave(x_bf[c], pair, slice(2, PACK), c in X_ON_VECTOR)
 
-        def turned_candidates(c):
-            for b in range(2):
-                block = slice(P * b, P * (b + 1))
-                ve = psum.tile([P, N], F32, name="ve")
-                nc.tensor.matmul_mx(
-                    ve[:], x_codes[c][:, block].bitcast(FP8X4), x_scales[c][:, block],
-                    wv_raw[:].bitcast(FP8X4), sv_raw[:], start=True, stop=True,
-                )
-                nc.scalar.activation(
-                    neg_t[c][:, b, :, :], ve[:].rearrange("j (m i) -> j i m", i=PACK), ACT.Tanh, scale=-1.0
-                )
-
-        def turned_gap(c):
-            for h in range(2):
-                bank = psum.tile([P, 2, 2 * P], F32, name="gap")
-                terms = [(src, i, b) for src in (res_t[c], neg_t[c]) for b in range(2) for i in range(2)]
-                for n, (src, i, b) in enumerate(terms):
-                    nc.tensor.matmul(
-                        bank[:, i, P * b : P * (b + 1)], src[:, b, 2 * h + i, :], ident[:],
-                        start=(n == 0), stop=(n == len(terms) - 1), is_transpose=True,
-                    )
-                gap[c, h] = bank
+        def quantise(c):
+            nc.vector.quantize_mx(x_codes[c][:].bitcast(FP8X4), x_scales[c][:], x_bf[c][:])
 
         def products(c):
             w = WIDTHS[c]
             per_bank = BANK // w
-            nc.vector.quantize_mx(x_codes[c][:].bitcast(FP8X4), x_scales[c][:], x_bf[c][:])
             if c in TURNED:
-                turned_candidates(c)
-            for i0 in range(0, PACK if c not in TURNED else 0, per_bank):
-                ve = psum.tile([P, per_bank, w], F32, name="ve")
-                for i in range(i0, i0 + per_bank):
+                for b in range(2):
+                    block = slice(P * b, P * (b + 1))
+                    ve = psum.tile([P, N], F32, name="ve")
                     nc.tensor.matmul_mx(
-                        ve[:, i - i0, :], wv[:, i, :].bitcast(FP8X4), sv[:, i, :],
-                        x_codes[c][:].bitcast(FP8X4), x_scales[c][:], start=True, stop=True,
+                        ve[:], x_codes[c][:, block].bitcast(FP8X4), x_scales[c][:, block],
+                        wv_raw[:].bitcast(FP8X4), sv_raw[:], start=True, stop=True,
                     )
-                nc.scalar.activation(cand[c][:, i0 : i0 + per_bank, :], ve[:], ACT.Tanh)
+                    nc.scalar.activation(
+                        neg_t[c][:, b, :, :], ve[:].rearrange("j (m i) -> j i m", i=PACK), ACT.Tanh, scale=-1.0
+                    )
             for i0 in range(0, PACK, per_bank):
+                if c not in TURNED:
+                    ve = psum.tile([P, per_bank, w], F32, name="ve")
+                    for i in range(i0, i0 + per_bank):
+                        nc.tensor.matmul_mx(
+                            ve[:, i - i0, :], wv[:, i, :].bitcast(FP8X4), sv[:, i, :],
+                            x_codes[c][:].bitcast(FP8X4), x_scales[c][:], start=True, stop=True,
+                        )
+                    nc.scalar.activation(cand[c][:, i0 : i0 + per_bank, :], ve[:], ACT.Tanh)
                 ke = psum.tile([P, per_bank, w], F32, name="ke")
                 for i in range(i0, i0 + per_bank):
                     nc.tensor.matmul_mx(
@@ -197,46 +213,53 @@ def tile_list_hwaytanhP_kernel(
             if c in TURNED:
                 turned_gap(c)
 
-        def blend(c):
-            halves = [slice(0, 2), slice(2, 4)]
-            if c in TURNED:
-                for n, h in enumerate(halves):
-                    nc.vector.tensor_tensor(step[c][:, h, :], gap[c, n][:], gate[c][:, h, :], ALU.mult)
-                for h in halves:
-                    nc.vector.tensor_tensor(y[c][:, h, :], res_sb[:, h, cols(c)], step[c][:, h, :], ALU.subtract)
-            else:
-                for h in halves:
-                    nc.vector.tensor_tensor(diff[c][:, h, :], cand[c][:, h, :], res_sb[:, h, cols(c)], ALU.subtract)
-                for h in halves:
-                    nc.vector.tensor_tensor(step[c][:, h, :], diff[c][:, h, :], gate[c][:, h, :], ALU.mult)
-                for h in halves:
-                    nc.vector.tensor_tensor(y[c][:, h, :], step[c][:, h, :], res_sb[:, h, cols(c)], ALU.add)
+        def parts(c):
+            return [slice(0, 2), slice(2, 4)] if c in SPLIT or c in TURNED else [slice(0, PACK)]
+
+        def subtract(c):
+            if c not in TURNED:
+                for h in parts(c):
+                    nc.vector.tensor_tensor(diff[c][:, h, :], res_sb[:, h, cols(c)], cand[c][:, h, :], ALU.subtract)
+
+        def scale(c):
+            for n, h in enumerate(parts(c)):
+                src = gap[c, n][:] if c in TURNED else diff[c][:, h, :]
+                nc.vector.tensor_tensor(step[c][:, h, :], src, gate[c][:, h, :], ALU.mult)
+
+        def add(c):
+            for h in parts(c):
+                nc.vector.tensor_tensor(y[c][:, h, :], res_sb[:, h, cols(c)], step[c][:, h, :], ALU.subtract)
             nc.sync.dma_start(out_rows[:, :, cols(c)], y[c][:])
+
+        def round_y(c):
             interleave(y_bf[c], y[c][:], slice(0, PACK), c in Y_ON_VECTOR)
 
         def hand_on(c):
             nc.vector.quantize_mx(y_codes[c][:].bitcast(FP8X4), y_scales[:, cols(c)], y_bf[c][:])
             nc.sync.dma_start(out_words[:, cols(c)], y_codes[c][:])
 
-        for i in range(2):
-            gather(early[:, i, :HALF], i, 0, HALF)
-            gather(early[:, i, HALF:], i, HALF, J)
-        nc.vector.tensor_copy(wv[:], wv_raw[:].rearrange("p (m i) -> p i m", i=PACK))
-        nc.vector.tensor_copy(sv[:], sv_raw[:].rearrange("p (m i) -> p i m", i=PACK))
-        for s in range(chunks + 4):
+        sort_k()
+        for h in range(SPREADS):
+            gather(early[:, 0, h * J // SPREADS : (h + 1) * J // SPREADS], 0, h * J // SPREADS, (h + 1) * J // SPREADS)
+        gather(early[:, 1, :], 1, 0, J)
+        sort_v()
+        for c in range(chunks):
+            interleave(x_bf[c], early[:, :, cols(c)], slice(0, 2), False)
+        gather(late[:, :J], 2, 0, J)
+        for s in range(chunks + 5):
             if s < chunks:
-                interleave(x_bf[s], early[:, :, cols(s)], slice(0, 2), False)
-                late = ring.tile([P, 2, WIDTHS[s]], F32, name="late")
-                for i in range(2, PACK):
-                    gather(late[:, i - 2, :], i, starts[s], starts[s] + WIDTHS[s])
-                interleave(x_bf[s], late[:], slice(2, PACK), s == 0)
+                front(s)
             if 0 <= s - 1 < chunks:
+                quantise(s - 1)
                 products(s - 1)
             if s in TURNED:
                 turn_res(s)
             if 0 <= s - 3 < chunks:
-                blend(s - 3)
+                subtract(s - 3)
+                scale(s - 3)
+                add(s - 3)
             if 0 <= s - 4 < chunks:
+                round_y(s - 4)
                 hand_on(s - 4)
         for q in range(4):
             queue = nc.sync if q % 2 == 0 else nc.scalar

@@ -30,6 +30,7 @@ SPLIT = (0, 1, 2, 3, 4)
 SLOTS = 2
 SLOT = 256
 TURNED = (3,)
+V_ROW = 4
 RES_PIECES = 4
 
 
@@ -52,12 +53,10 @@ def tile_list_hwaytanhP_kernel(
         offsets = keep.tile([P, J // GROUP], U16, name="offsets")
         wk_raw = keep.tile([P, 2 * N], U8, name="wk_raw", align_bytes=64)
         wv_raw = keep.tile([P, N], I32, name="wv_raw", align_bytes=64)
-        sk_raw = keep.tile([P, N], U8, name="sk_raw", align_bytes=64)
-        sv_raw = keep.tile([P, N], U8, name="sv_raw", align_bytes=64)
+        scales_raw = keep.tile([P, N], U8, name="scales_raw", align_bytes=64)
         wk = keep.tile([P, PACK, 2 * P], U8, name="wk", align_bytes=64)
         wv = keep.tile([P, PACK, P], I32, name="wv", align_bytes=64)
-        sk = keep.tile([P, PACK, P], U8, name="sk", align_bytes=64)
-        sv = keep.tile([P, PACK, P], U8, name="sv", align_bytes=64)
+        scales = keep.tile([P, PACK, P], U8, name="scales", align_bytes=64)
         bias = keep.tile([P, PACK], F32, name="bias")
         warm = keep.tile([P, 8], F32, name="warm")
         warm_out = keep.tile([P, 8], F32, name="warm_out")
@@ -69,25 +68,25 @@ def tile_list_hwaytanhP_kernel(
         wgt_wide = [keep.tile([P, HEADS // SPREADS, P], F32, name="wgt_wide%d" % h) for h in range(SPREADS)]
         ident = keep.tile([P, P], F32, name="ident")
 
-        nc.vector.memset(sk_raw[:].bitcast(I32), 0)
+        nc.vector.memset(scales_raw[:].bitcast(I32), 0)
         nc.vector.memset(warm[:], 0.0)
         nc.vector.memset(wgt_rows[P // 2 :, :], 0.0)
-        nc.vector.memset(sv_raw[:].bitcast(I32), 0)
         make_identity(nc, ident[:])
 
-        def load_scales(queue, tile, rows):
+        def load_scales(queue, first, rows):
             for q in range(4):
-                queue.dma_start(tile[32 * q : 32 * q + 4, :].bitcast(I32), rows[4 * q : 4 * q + 4, :].bitcast(I32))
+                dst = scales_raw[32 * q + first : 32 * q + first + 4, :]
+                queue.dma_start(dst.bitcast(I32), rows[4 * q : 4 * q + 4, :].bitcast(I32))
 
         one_row = wgt.rearrange("(g r) j -> g r j", r=GROUP)[:, 0, :]
         nc.sync.dma_start(wgt_rows[: P // 2, :], one_row.rearrange("g (s j) -> g s j", j=P))
-        nc.sync.dma_start(wk_raw[:].bitcast(I32), wk_words[0].bitcast(I32))
-        load_scales(nc.sync, sk_raw, wk_scales[0])
         nc.sync.dma_start(offsets[:], offs)
         nc.sync.dma_start(planes[0][:], x_planes[:, 0, :])
+        load_scales(nc.sync, 0, wk_scales[0])
         nc.sync.dma_start(planes[1][:], x_planes[:, 1, :])
+        load_scales(nc.sync, V_ROW, wv_scales[0])
+        nc.sync.dma_start(wk_raw[:].bitcast(I32), wk_words[0].bitcast(I32))
         nc.sync.dma_start(wv_raw[:], wv_words[0].rearrange("p n i -> p (n i)").bitcast(I32))
-        load_scales(nc.sync, sv_raw, wv_scales[0])
         nc.sync.dma_start(planes[2][:], x_planes[:, 2, :])
         nc.sync.dma_start(planes[3][:], x_planes[:, 3, :])
         nc.sync.dma_start(bias[:], bg.rearrange("(p i) -> p i", i=PACK))
@@ -112,11 +111,12 @@ def tile_list_hwaytanhP_kernel(
 
         def sort_k():
             nc.vector.tensor_copy(wk[:].bitcast(U16), wk_raw[:].bitcast(U16).rearrange("p (m i) -> p i m", i=PACK))
-            nc.vector.tensor_copy(sk[:], sk_raw[:].rearrange("p (m i) -> p i m", i=PACK))
 
         def sort_v():
             nc.vector.tensor_copy(wv[:], wv_raw[:].rearrange("p (m i) -> p i m", i=PACK))
-            nc.vector.tensor_copy(sv[:], sv_raw[:].rearrange("p (m i) -> p i m", i=PACK))
+
+        def sort_scales():
+            nc.vector.tensor_copy(scales[:], scales_raw[:].rearrange("p (m i) -> p i m", i=PACK))
 
         early = keep.tile([P, 2, J], F32, name="early")
         late = keep.tile([P, 2 * (J + SLOTS * SLOT)], F32, name="late")
@@ -188,7 +188,7 @@ def tile_list_hwaytanhP_kernel(
                     ve = psum.tile([P, N], F32, name="ve")
                     nc.tensor.matmul_mx(
                         ve[:], x_codes[c][:, block].bitcast(FP8X4), x_scales[c][:, block],
-                        wv_raw[:].bitcast(FP8X4), sv_raw[:], start=True, stop=True,
+                        wv_raw[:].bitcast(FP8X4), scales_raw[V_ROW:, :], start=True, stop=True,
                     )
                     nc.scalar.activation(
                         neg_t[c][:, b, :, :], ve[:].rearrange("j (m i) -> j i m", i=PACK), ACT.Tanh, scale=-1.0
@@ -198,14 +198,14 @@ def tile_list_hwaytanhP_kernel(
                     ve = psum.tile([P, per_bank, w], F32, name="ve")
                     for i in range(i0, i0 + per_bank):
                         nc.tensor.matmul_mx(
-                            ve[:, i - i0, :], wv[:, i, :].bitcast(FP8X4), sv[:, i, :],
+                            ve[:, i - i0, :], wv[:, i, :].bitcast(FP8X4), scales[V_ROW:, i, :],
                             x_codes[c][:].bitcast(FP8X4), x_scales[c][:], start=True, stop=True,
                         )
                     nc.scalar.activation(cand[c][:, i0 : i0 + per_bank, :], ve[:], ACT.Tanh)
                 ke = psum.tile([P, per_bank, w], F32, name="ke")
                 for i in range(i0, i0 + per_bank):
                     nc.tensor.matmul_mx(
-                        ke[:, i - i0, :], wk[:, i, :].bitcast(FP4X4), sk[:, i, :],
+                        ke[:, i - i0, :], wk[:, i, :].bitcast(FP4X4), scales[:, i, :],
                         x_codes[c][:].bitcast(FP8X4), x_scales[c][:], start=True, stop=True,
                     )
                 for i in range(i0, i0 + per_bank):
@@ -238,10 +238,11 @@ def tile_list_hwaytanhP_kernel(
             nc.vector.quantize_mx(y_codes[c][:].bitcast(FP8X4), y_scales[:, cols(c)], y_bf[c][:])
             nc.sync.dma_start(out_words[:, cols(c)], y_codes[c][:])
 
-        sort_k()
         for h in range(SPREADS):
             gather(early[:, 0, h * J // SPREADS : (h + 1) * J // SPREADS], 0, h * J // SPREADS, (h + 1) * J // SPREADS)
         gather(early[:, 1, :], 1, 0, J)
+        sort_scales()
+        sort_k()
         sort_v()
         for c in range(chunks):
             interleave(x_bf[c], early[:, :, cols(c)], slice(0, 2), False)
@@ -258,9 +259,9 @@ def tile_list_hwaytanhP_kernel(
                 subtract(s - 3)
                 scale(s - 3)
                 add(s - 3)
-            if 0 <= s - 4 < chunks:
-                round_y(s - 4)
-                hand_on(s - 4)
+            if 0 <= s - 5 < chunks:
+                round_y(s - 5)
+                hand_on(s - 5)
         for q in range(4):
             queue = nc.sync if q % 2 == 0 else nc.scalar
             queue.dma_start(

@@ -162,8 +162,8 @@ def tile_list_hwaytanhP_kernel(
             nc.vector.tensor_tensor(dst, planes[i][:].indirect(entries), wgt_sb[:, j0:j1], ALU.mult)
 
         def interleave(dst, src, rows, on_vector):
-            dst_view = dst[:].rearrange("p (u e i) -> p u i e", e=2, i=PACK)[:, :, rows, :]
-            src_view = src.rearrange("p i (u e) -> p u i e", e=2)
+            dst_view = dst[:].rearrange("p (u e i) -> p u i e", e=4, i=PACK)[:, :, rows, :]
+            src_view = src.rearrange("p i (u e) -> p u i e", e=4)
             if on_vector:
                 nc.vector.tensor_copy(dst_view, src_view)
             else:
@@ -210,8 +210,6 @@ def tile_list_hwaytanhP_kernel(
                     )
                 for i in range(i0, i0 + per_bank):
                     nc.scalar.activation(gate[c][:, i, :], ke[:, i - i0, :], ACT.Sigmoid, bias=bias[:, i : i + 1])
-            if c in TURNED:
-                turned_gap(c)
 
         def parts(c):
             return [slice(0, 2), slice(2, 4)] if c in SPLIT or c in TURNED else [slice(0, PACK)]
@@ -255,6 +253,8 @@ def tile_list_hwaytanhP_kernel(
                 products(s - 1)
             if s in TURNED:
                 turn_res(s)
+            if s - 2 in TURNED:
+                turned_gap(s - 2)
             if 0 <= s - 3 < chunks:
                 subtract(s - 3)
                 scale(s - 3)

@@ -25,13 +25,14 @@ HALF = J // 2
 WIDTHS = [128, 256, 256, 256, 128]
 X_ON_VECTOR = ()
 Y_ON_VECTOR = (4,)
+EARLY_TURNED = (3,)
+LATE_TURNED = ()
+TURNED = EARLY_TURNED + LATE_TURNED
 SPREADS = 4
-SPLIT = (0, 1, 2, 3, 4)
-SLOTS = 2
+SLOTS = 3
 SLOT = 256
-TURNED = (3,)
 V_ROW = 4
-RES_PIECES = 4
+RUN = 2
 
 
 def tile_list_hwaytanhP_kernel(
@@ -62,7 +63,7 @@ def tile_list_hwaytanhP_kernel(
         warm_out = keep.tile([P, 8], F32, name="warm_out")
         planes = [keep.tile([P, T], F32, name="plane%d" % i) for i in range(PACK)]
         wgt_sb = keep.tile([P, J], F32, name="wgt_sb")
-        res_sb = keep.tile([P, PACK, J], F32, name="res_sb")
+        res_sb = [keep.tile([P, PACK, w], F32, name="res%d" % c) for c, w in enumerate(WIDTHS)]
         y_scales = keep.tile([P, J], U8, name="y_scales", align_bytes=64)
         wgt_rows = keep.tile([P, P], F32, name="wgt_rows")
         wgt_wide = [keep.tile([P, HEADS // SPREADS, P], F32, name="wgt_wide%d" % h) for h in range(SPREADS)]
@@ -73,33 +74,41 @@ def tile_list_hwaytanhP_kernel(
         nc.vector.memset(wgt_rows[P // 2 :, :], 0.0)
         make_identity(nc, ident[:])
 
+        def cols(c):
+            return slice(starts[c], starts[c] + WIDTHS[c])
+
         def load_scales(queue, first, rows):
             for q in range(4):
                 dst = scales_raw[32 * q + first : 32 * q + first + 4, :]
                 queue.dma_start(dst.bitcast(I32), rows[4 * q : 4 * q + 4, :].bitcast(I32))
 
+        def load_res(c):
+            nc.sync.dma_start(res_sb[c][:], res_rows[:, :, cols(c)])
+
         one_row = wgt.rearrange("(g r) j -> g r j", r=GROUP)[:, 0, :]
         nc.sync.dma_start(wgt_rows[: P // 2, :], one_row.rearrange("g (s j) -> g s j", j=P))
         nc.sync.dma_start(offsets[:], offs)
+        nc.sync.dma_start(wk_raw[:].bitcast(I32), wk_words[0].bitcast(I32))
         nc.sync.dma_start(planes[0][:], x_planes[:, 0, :])
         load_scales(nc.sync, 0, wk_scales[0])
         nc.sync.dma_start(planes[1][:], x_planes[:, 1, :])
+        load_res(3)
         load_scales(nc.sync, V_ROW, wv_scales[0])
-        nc.sync.dma_start(wk_raw[:].bitcast(I32), wk_words[0].bitcast(I32))
         nc.sync.dma_start(wv_raw[:], wv_words[0].rearrange("p n i -> p (n i)").bitcast(I32))
         nc.sync.dma_start(planes[2][:], x_planes[:, 2, :])
         nc.sync.dma_start(planes[3][:], x_planes[:, 3, :])
         nc.sync.dma_start(bias[:], bg.rearrange("(p i) -> p i", i=PACK))
-        for a in range(RES_PIECES):
-            piece = slice(a * J // RES_PIECES, (a + 1) * J // RES_PIECES)
-            nc.sync.dma_start(res_sb[:, :, piece], res_rows[:, :, piece])
+        load_res(0)
+        load_res(1)
+        load_res(2)
+        load_res(4)
         nc.scalar.activation(warm_out[:], warm[:], ACT.Sigmoid)
 
-        turned = psum.tile([P, 2, HEADS, HEADS], F32, name="ke")
-        nc.tensor.transpose(turned[:].rearrange("j z g s -> j (z g s)"), wgt_rows[:], ident[:])
+        heads_t = psum.tile([P, 2, HEADS, HEADS], F32, name="ke")
+        nc.tensor.transpose(heads_t[:].rearrange("j z g s -> j (z g s)"), wgt_rows[:], ident[:])
         for h in range(SPREADS):
             per = HEADS // SPREADS
-            heads = turned[:, 0, :, per * h : per * (h + 1)].rearrange("j g s -> j s g")
+            heads = heads_t[:, 0, :, per * h : per * (h + 1)].rearrange("j g s -> j s g")
             nc.scalar.copy(
                 wgt_wide[h][:].rearrange("j s (g r) -> j s g r", r=GROUP),
                 heads.unsqueeze(3).to_broadcast([P, per, HEADS, GROUP]),
@@ -109,61 +118,39 @@ def tile_list_hwaytanhP_kernel(
                 nc.tensor.transpose(spread[:, s, :], wgt_wide[h][:, s, :], ident[:])
             nc.scalar.copy(wgt_sb[:, per * P * h : per * P * (h + 1)], spread[:].rearrange("p s j -> p (s j)"))
 
-        def sort_k():
-            nc.vector.tensor_copy(wk[:].bitcast(U16), wk_raw[:].bitcast(U16).rearrange("p (m i) -> p i m", i=PACK))
-
-        def sort_v():
-            nc.vector.tensor_copy(wv[:], wv_raw[:].rearrange("p (m i) -> p i m", i=PACK))
-
-        def sort_scales():
+        def sort_weights():
             nc.vector.tensor_copy(scales[:], scales_raw[:].rearrange("p (m i) -> p i m", i=PACK))
+            nc.vector.tensor_copy(wv[:], wv_raw[:].rearrange("p (m i) -> p i m", i=PACK))
 
         early = keep.tile([P, 2, J], F32, name="early")
         late = keep.tile([P, 2 * (J + SLOTS * SLOT)], F32, name="late")
         x_bf = [keep.tile([P, PACK * w], BF16, name="x_bf%d" % c, align_bytes=64) for c, w in enumerate(WIDTHS)]
         x_codes = [keep.tile([P, w], I32, name="x_codes%d" % c, align_bytes=64) for c, w in enumerate(WIDTHS)]
         x_scales = [keep.tile([P, w], U8, name="x_scales%d" % c, align_bytes=64) for c, w in enumerate(WIDTHS)]
-        cand = [keep.tile([P, PACK, w], F32, name="cand%d" % c) for c, w in enumerate(WIDTHS)]
+        cand = [keep.tile([P, PACK * w], F32, name="cand%d" % c) for c, w in enumerate(WIDTHS)]
         gate = [keep.tile([P, PACK, w], F32, name="gate%d" % c) for c, w in enumerate(WIDTHS)]
-        diff = [keep.tile([P, PACK, w], F32, name="diff%d" % c) for c, w in enumerate(WIDTHS)]
+        diff = {c: keep.tile([P, PACK, w], F32, name="diff%d" % c) for c, w in enumerate(WIDTHS) if c not in TURNED}
+        res_t = {c: keep.tile([P, PACK * WIDTHS[c]], F32, name="res_t%d" % c) for c in TURNED}
         step = [keep.tile([P, PACK, w], F32, name="step%d" % c) for c, w in enumerate(WIDTHS)]
         y = [keep.tile([P, PACK, w], F32, name="y%d" % c) for c, w in enumerate(WIDTHS)]
         y_bf = [keep.tile([P, PACK * w], BF16, name="y_bf%d" % c, align_bytes=64) for c, w in enumerate(WIDTHS)]
         y_codes = [keep.tile([P, w], I32, name="y_codes%d" % c, align_bytes=64) for c, w in enumerate(WIDTHS)]
-
-        res_t = {c: keep.tile([P, 2, PACK, P], F32, name="res_t%d" % c) for c in TURNED}
-        neg_t = {c: keep.tile([P, 2, PACK, P], F32, name="neg_t%d" % c) for c in TURNED}
         gap = {}
 
-        def turn_res(c):
-            for b in range(2):
-                bank = psum.tile([P, PACK, P], F32, name="rt")
-                j0 = starts[c] + P * b
-                for i in range(PACK):
-                    nc.tensor.transpose(bank[:, i, :], res_sb[:, i, j0 : j0 + P], ident[:])
-                nc.scalar.copy(res_t[c][:, b, :, :], bank[:])
+        def by_block(tile):
+            return tile[:].rearrange("j (b i m) -> j b i m", i=PACK, m=P)
 
-        def turned_gap(c):
-            for h in range(2):
-                bank = psum.tile([P, 2, 2 * P], F32, name="gap")
-                terms = [(src, i, b) for src in (res_t[c], neg_t[c]) for b in range(2) for i in range(2)]
-                for n, (src, i, b) in enumerate(terms):
-                    nc.tensor.matmul(
-                        bank[:, i, P * b : P * (b + 1)], src[:, b, 2 * h + i, :], ident[:],
-                        start=(n == 0), stop=(n == len(terms) - 1), is_transpose=True,
-                    )
-                gap[c, h] = bank
-
-        def cols(c):
-            return slice(starts[c], starts[c] + WIDTHS[c])
+        def banks_of(c):
+            per_bank = BANK // WIDTHS[c]
+            return [range(i0, i0 + per_bank) for i0 in range(0, PACK, per_bank)]
 
         def gather(dst, i, j0, j1):
             entries = offsets[:, j0 // GROUP : j1 // GROUP]
             nc.vector.tensor_tensor(dst, planes[i][:].indirect(entries), wgt_sb[:, j0:j1], ALU.mult)
 
         def interleave(dst, src, rows, on_vector):
-            dst_view = dst[:].rearrange("p (u e i) -> p u i e", e=4, i=PACK)[:, :, rows, :]
-            src_view = src.rearrange("p i (u e) -> p u i e", e=4)
+            dst_view = dst[:].rearrange("p (u e i) -> p u i e", e=RUN, i=PACK)[:, :, rows, :]
+            src_view = src.rearrange("p i (u e) -> p u i e", e=RUN)
             if on_vector:
                 nc.vector.tensor_copy(dst_view, src_view)
             else:
@@ -176,14 +163,31 @@ def tile_list_hwaytanhP_kernel(
             pair = late[:, starts[c] : 2 * slot - starts[c]].rearrange("p (r x) -> p r x", r=2)[:, :, :w]
             interleave(x_bf[c], pair, slice(2, PACK), c in X_ON_VECTOR)
 
+        def turn_res(c):
+            for b in range(WIDTHS[c] // P):
+                bank = psum.tile([P, PACK, P], F32, name="spare")
+                for i in range(PACK):
+                    nc.tensor.transpose(bank[:, i, :], res_sb[c][:, i, P * b : P * (b + 1)], ident[:])
+                nc.scalar.copy(by_block(res_t[c])[:, b, :, :], bank[:])
+
+        def sum_terms(c, src, first):
+            for n, rows in enumerate(banks_of(c)):
+                if first:
+                    gap[c, n] = psum.tile([P, len(rows), WIDTHS[c]], F32, name="gap" if c in EARLY_TURNED else "spare")
+                terms = [(b, i) for b in range(WIDTHS[c] // P) for i in rows]
+                for m, (b, i) in enumerate(terms):
+                    nc.tensor.matmul(
+                        gap[c, n][:, i - rows[0], P * b : P * (b + 1)], by_block(src)[:, b, i, :], ident[:],
+                        start=(first and m == 0), stop=(not first and m == len(terms) - 1), is_transpose=True,
+                    )
+
         def quantise(c):
             nc.vector.quantize_mx(x_codes[c][:].bitcast(FP8X4), x_scales[c][:], x_bf[c][:])
 
         def products(c):
             w = WIDTHS[c]
-            per_bank = BANK // w
             if c in TURNED:
-                for b in range(2):
+                for b in range(w // P):
                     block = slice(P * b, P * (b + 1))
                     ve = psum.tile([P, N], F32, name="ve")
                     nc.tensor.matmul_mx(
@@ -191,42 +195,41 @@ def tile_list_hwaytanhP_kernel(
                         wv_raw[:].bitcast(FP8X4), scales_raw[V_ROW:, :], start=True, stop=True,
                     )
                     nc.scalar.activation(
-                        neg_t[c][:, b, :, :], ve[:].rearrange("j (m i) -> j i m", i=PACK), ACT.Tanh, scale=-1.0
+                        by_block(cand[c])[:, b, :, :], ve[:].rearrange("j (m i) -> j i m", i=PACK), ACT.Tanh, scale=-1.0
                     )
-            for i0 in range(0, PACK, per_bank):
+            for rows in banks_of(c):
                 if c not in TURNED:
-                    ve = psum.tile([P, per_bank, w], F32, name="ve")
-                    for i in range(i0, i0 + per_bank):
+                    ve = psum.tile([P, len(rows), w], F32, name="ve")
+                    for i in rows:
                         nc.tensor.matmul_mx(
-                            ve[:, i - i0, :], wv[:, i, :].bitcast(FP8X4), scales[V_ROW:, i, :],
+                            ve[:, i - rows[0], :], wv[:, i, :].bitcast(FP8X4), scales[V_ROW:, i, :],
                             x_codes[c][:].bitcast(FP8X4), x_scales[c][:], start=True, stop=True,
                         )
-                    nc.scalar.activation(cand[c][:, i0 : i0 + per_bank, :], ve[:], ACT.Tanh)
-                ke = psum.tile([P, per_bank, w], F32, name="ke")
-                for i in range(i0, i0 + per_bank):
+                    part = cand[c][:, w * rows[0] : w * (rows[-1] + 1)]
+                    nc.scalar.activation(part, ve[:].rearrange("p i j -> p (i j)"), ACT.Tanh)
+                ke = psum.tile([P, len(rows), w], F32, name="ke")
+                for i in rows:
                     nc.tensor.matmul_mx(
-                        ke[:, i - i0, :], wk[:, i, :].bitcast(FP4X4), scales[:, i, :],
+                        ke[:, i - rows[0], :], wk[:, i, :].bitcast(FP4X4), scales[:, i, :],
                         x_codes[c][:].bitcast(FP8X4), x_scales[c][:], start=True, stop=True,
                     )
-                for i in range(i0, i0 + per_bank):
-                    nc.scalar.activation(gate[c][:, i, :], ke[:, i - i0, :], ACT.Sigmoid, bias=bias[:, i : i + 1])
+                for i in rows:
+                    nc.scalar.activation(gate[c][:, i, :], ke[:, i - rows[0], :], ACT.Sigmoid, bias=bias[:, i : i + 1])
 
-        def parts(c):
-            return [slice(0, 2), slice(2, 4)] if c in SPLIT or c in TURNED else [slice(0, PACK)]
-
-        def subtract(c):
-            if c not in TURNED:
-                for h in parts(c):
-                    nc.vector.tensor_tensor(diff[c][:, h, :], res_sb[:, h, cols(c)], cand[c][:, h, :], ALU.subtract)
-
-        def scale(c):
-            for n, h in enumerate(parts(c)):
-                src = gap[c, n][:] if c in TURNED else diff[c][:, h, :]
+        def blend(c):
+            w = WIDTHS[c]
+            halves = [slice(0, 2), slice(2, 4)]
+            if c in TURNED:
+                gaps = [gap[c, n][:] for n in range(2)] if w > P else [gap[c, 0][:, h, :] for h in halves]
+            else:
+                rows = cand[c][:].rearrange("p (i j) -> p i j", i=PACK)
+                for h in halves:
+                    nc.vector.tensor_tensor(diff[c][:, h, :], res_sb[c][:, h, :], rows[:, h, :], ALU.subtract)
+                gaps = [diff[c][:, h, :] for h in halves]
+            for h, src in zip(halves, gaps):
                 nc.vector.tensor_tensor(step[c][:, h, :], src, gate[c][:, h, :], ALU.mult)
-
-        def add(c):
-            for h in parts(c):
-                nc.vector.tensor_tensor(y[c][:, h, :], res_sb[:, h, cols(c)], step[c][:, h, :], ALU.subtract)
+            for h in halves:
+                nc.vector.tensor_tensor(y[c][:, h, :], res_sb[c][:, h, :], step[c][:, h, :], ALU.subtract)
             nc.sync.dma_start(out_rows[:, :, cols(c)], y[c][:])
 
         def round_y(c):
@@ -236,12 +239,14 @@ def tile_list_hwaytanhP_kernel(
             nc.vector.quantize_mx(y_codes[c][:].bitcast(FP8X4), y_scales[:, cols(c)], y_bf[c][:])
             nc.sync.dma_start(out_words[:, cols(c)], y_codes[c][:])
 
+        nc.vector.tensor_copy(wk[:].bitcast(U16), wk_raw[:].bitcast(U16).rearrange("p (m i) -> p i m", i=PACK))
         for h in range(SPREADS):
             gather(early[:, 0, h * J // SPREADS : (h + 1) * J // SPREADS], 0, h * J // SPREADS, (h + 1) * J // SPREADS)
+        for c in EARLY_TURNED:
+            turn_res(c)
+            sum_terms(c, res_t[c], True)
         gather(early[:, 1, :], 1, 0, J)
-        sort_scales()
-        sort_k()
-        sort_v()
+        sort_weights()
         for c in range(chunks):
             interleave(x_bf[c], early[:, :, cols(c)], slice(0, 2), False)
         gather(late[:, :J], 2, 0, J)
@@ -250,15 +255,14 @@ def tile_list_hwaytanhP_kernel(
                 front(s)
             if 0 <= s - 1 < chunks:
                 quantise(s - 1)
+                if s - 1 in LATE_TURNED:
+                    turn_res(s - 1)
+                    sum_terms(s - 1, res_t[s - 1], True)
                 products(s - 1)
-            if s in TURNED:
-                turn_res(s)
-            if s - 2 in TURNED:
-                turned_gap(s - 2)
+                if s - 1 in TURNED:
+                    sum_terms(s - 1, cand[s - 1], False)
             if 0 <= s - 3 < chunks:
-                subtract(s - 3)
-                scale(s - 3)
-                add(s - 3)
+                blend(s - 3)
             if 0 <= s - 5 < chunks:
                 round_y(s - 5)
                 hand_on(s - 5)

@@ -25,8 +25,8 @@ HALF = J // 2
 WIDTHS = [128, 256, 256, 256, 128]
 X_ON_VECTOR = ()
 Y_ON_VECTOR = (4,)
-EARLY_TURNED = (3,)
-LATE_TURNED = ()
+EARLY_TURNED = ()
+LATE_TURNED = (3,)
 TURNED = EARLY_TURNED + LATE_TURNED
 SPREADS = 4
 SLOTS = 3
@@ -88,19 +88,19 @@ def tile_list_hwaytanhP_kernel(
         one_row = wgt.rearrange("(g r) j -> g r j", r=GROUP)[:, 0, :]
         nc.sync.dma_start(wgt_rows[: P // 2, :], one_row.rearrange("g (s j) -> g s j", j=P))
         nc.sync.dma_start(offsets[:], offs)
-        nc.sync.dma_start(wk_raw[:].bitcast(I32), wk_words[0].bitcast(I32))
         nc.sync.dma_start(planes[0][:], x_planes[:, 0, :])
         load_scales(nc.sync, 0, wk_scales[0])
         nc.sync.dma_start(planes[1][:], x_planes[:, 1, :])
-        load_res(3)
         load_scales(nc.sync, V_ROW, wv_scales[0])
-        nc.sync.dma_start(wv_raw[:], wv_words[0].rearrange("p n i -> p (n i)").bitcast(I32))
+        nc.sync.dma_start(bias[:], bg.rearrange("(p i) -> p i", i=PACK))
         nc.sync.dma_start(planes[2][:], x_planes[:, 2, :])
         nc.sync.dma_start(planes[3][:], x_planes[:, 3, :])
-        nc.sync.dma_start(bias[:], bg.rearrange("(p i) -> p i", i=PACK))
+        nc.sync.dma_start(wk_raw[:].bitcast(I32), wk_words[0].bitcast(I32))
+        nc.sync.dma_start(wv_raw[:], wv_words[0].rearrange("p n i -> p (n i)").bitcast(I32))
         load_res(0)
         load_res(1)
         load_res(2)
+        load_res(3)
         load_res(4)
         nc.scalar.activation(warm_out[:], warm[:], ACT.Sigmoid)
 
@@ -118,8 +118,11 @@ def tile_list_hwaytanhP_kernel(
                 nc.tensor.transpose(spread[:, s, :], wgt_wide[h][:, s, :], ident[:])
             nc.scalar.copy(wgt_sb[:, per * P * h : per * P * (h + 1)], spread[:].rearrange("p s j -> p (s j)"))
 
-        def sort_weights():
+        def sort_scales():
             nc.vector.tensor_copy(scales[:], scales_raw[:].rearrange("p (m i) -> p i m", i=PACK))
+
+        def sort_words():
+            nc.vector.tensor_copy(wk[:].bitcast(U16), wk_raw[:].bitcast(U16).rearrange("p (m i) -> p i m", i=PACK))
             nc.vector.tensor_copy(wv[:], wv_raw[:].rearrange("p (m i) -> p i m", i=PACK))
 
         early = keep.tile([P, 2, J], F32, name="early")
@@ -239,20 +242,21 @@ def tile_list_hwaytanhP_kernel(
             nc.vector.quantize_mx(y_codes[c][:].bitcast(FP8X4), y_scales[:, cols(c)], y_bf[c][:])
             nc.sync.dma_start(out_words[:, cols(c)], y_codes[c][:])
 
-        nc.vector.tensor_copy(wk[:].bitcast(U16), wk_raw[:].bitcast(U16).rearrange("p (m i) -> p i m", i=PACK))
         for h in range(SPREADS):
             gather(early[:, 0, h * J // SPREADS : (h + 1) * J // SPREADS], 0, h * J // SPREADS, (h + 1) * J // SPREADS)
         for c in EARLY_TURNED:
             turn_res(c)
             sum_terms(c, res_t[c], True)
         gather(early[:, 1, :], 1, 0, J)
-        sort_weights()
+        sort_scales()
         for c in range(chunks):
             interleave(x_bf[c], early[:, :, cols(c)], slice(0, 2), False)
         gather(late[:, :J], 2, 0, J)
         for s in range(chunks + 5):
             if s < chunks:
                 front(s)
+            if s == 1:
+                sort_words()
             if 0 <= s - 1 < chunks:
                 quantise(s - 1)
                 if s - 1 in LATE_TURNED:

@@ -28,7 +28,7 @@ Y_ON_VECTOR = (4,)
 EARLY_TURNED = ()
 LATE_TURNED = (3,)
 TURNED = EARLY_TURNED + LATE_TURNED
-SPREADS = 4
+SPREADS = [(0, 2), (5, 8), (2, 3), (3, 5)]
 SLOTS = 3
 SLOT = 256
 V_ROW = 4
@@ -66,7 +66,7 @@ def tile_list_hwaytanhP_kernel(
         res_sb = [keep.tile([P, PACK, w], F32, name="res%d" % c) for c, w in enumerate(WIDTHS)]
         y_scales = keep.tile([P, J], U8, name="y_scales", align_bytes=64)
         wgt_rows = keep.tile([P, P], F32, name="wgt_rows")
-        wgt_wide = [keep.tile([P, HEADS // SPREADS, P], F32, name="wgt_wide%d" % h) for h in range(SPREADS)]
+        wgt_wide = keep.tile([P, HEADS, P], F32, name="wgt_wide")
         ident = keep.tile([P, P], F32, name="ident")
 
         nc.vector.memset(scales_raw[:].bitcast(I32), 0)
@@ -106,17 +106,16 @@ def tile_list_hwaytanhP_kernel(
 
         heads_t = psum.tile([P, 2, HEADS, HEADS], F32, name="ke")
         nc.tensor.transpose(heads_t[:].rearrange("j z g s -> j (z g s)"), wgt_rows[:], ident[:])
-        for h in range(SPREADS):
-            per = HEADS // SPREADS
-            heads = heads_t[:, 0, :, per * h : per * (h + 1)].rearrange("j g s -> j s g")
+        for b0, b1 in SPREADS:
+            heads = heads_t[:, 0, :, b0:b1].rearrange("j g s -> j s g")
             nc.scalar.copy(
-                wgt_wide[h][:].rearrange("j s (g r) -> j s g r", r=GROUP),
-                heads.unsqueeze(3).to_broadcast([P, per, HEADS, GROUP]),
+                wgt_wide[:, b0:b1, :].rearrange("j s (g r) -> j s g r", r=GROUP),
+                heads.unsqueeze(3).to_broadcast([P, b1 - b0, HEADS, GROUP]),
             )
-            spread = psum.tile([P, per, P], F32, name="ve")
-            for s in range(per):
-                nc.tensor.transpose(spread[:, s, :], wgt_wide[h][:, s, :], ident[:])
-            nc.scalar.copy(wgt_sb[:, per * P * h : per * P * (h + 1)], spread[:].rearrange("p s j -> p (s j)"))
+            spread = psum.tile([P, b1 - b0, P], F32, name="ve")
+            for s in range(b0, b1):
+                nc.tensor.transpose(spread[:, s - b0, :], wgt_wide[:, s, :], ident[:])
+            nc.scalar.copy(wgt_sb[:, P * b0 : P * b1], spread[:].rearrange("p s j -> p (s j)"))
 
         def sort_scales():
             nc.vector.tensor_copy(scales[:], scales_raw[:].rearrange("p (m i) -> p i m", i=PACK))
@@ -127,7 +126,8 @@ def tile_list_hwaytanhP_kernel(
 
         early = keep.tile([P, 2, J], F32, name="early")
         late = keep.tile([P, 2 * (J + SLOTS * SLOT)], F32, name="late")
-        x_bf = [keep.tile([P, PACK * w], BF16, name="x_bf%d" % c, align_bytes=64) for c, w in enumerate(WIDTHS)]
+        x_all = keep.tile([P, PACK * J], BF16, name="x_all", align_bytes=64)
+        x_bf = [x_all[:, PACK * starts[c] : PACK * (starts[c] + w)] for c, w in enumerate(WIDTHS)]
         x_codes = [keep.tile([P, w], I32, name="x_codes%d" % c, align_bytes=64) for c, w in enumerate(WIDTHS)]
         x_scales = [keep.tile([P, w], U8, name="x_scales%d" % c, align_bytes=64) for c, w in enumerate(WIDTHS)]
         cand = [keep.tile([P, PACK * w], F32, name="cand%d" % c) for c, w in enumerate(WIDTHS)]
@@ -152,7 +152,7 @@ def tile_list_hwaytanhP_kernel(
             nc.vector.tensor_tensor(dst, planes[i][:].indirect(entries), wgt_sb[:, j0:j1], ALU.mult)
 
         def interleave(dst, src, rows, on_vector):
-            dst_view = dst[:].rearrange("p (u e i) -> p u i e", e=RUN, i=PACK)[:, :, rows, :]
+            dst_view = dst.rearrange("p (u e i) -> p u i e", e=RUN, i=PACK)[:, :, rows, :]
             src_view = src.rearrange("p i (u e) -> p u i e", e=RUN)
             if on_vector:
                 nc.vector.tensor_copy(dst_view, src_view)
@@ -185,7 +185,7 @@ def tile_list_hwaytanhP_kernel(
                     )
 
         def quantise(c):
-            nc.vector.quantize_mx(x_codes[c][:].bitcast(FP8X4), x_scales[c][:], x_bf[c][:])
+            nc.vector.quantize_mx(x_codes[c][:].bitcast(FP8X4), x_scales[c][:], x_bf[c])
 
         def products(c):
             w = WIDTHS[c]
@@ -236,21 +236,21 @@ def tile_list_hwaytanhP_kernel(
             nc.sync.dma_start(out_rows[:, :, cols(c)], y[c][:])
 
         def round_y(c):
-            interleave(y_bf[c], y[c][:], slice(0, PACK), c in Y_ON_VECTOR)
+            interleave(y_bf[c][:], y[c][:], slice(0, PACK), c in Y_ON_VECTOR)
 
         def hand_on(c):
             nc.vector.quantize_mx(y_codes[c][:].bitcast(FP8X4), y_scales[:, cols(c)], y_bf[c][:])
             nc.sync.dma_start(out_words[:, cols(c)], y_codes[c][:])
 
-        for h in range(SPREADS):
-            gather(early[:, 0, h * J // SPREADS : (h + 1) * J // SPREADS], 0, h * J // SPREADS, (h + 1) * J // SPREADS)
+        for b0, b1 in SPREADS:
+            gather(early[:, 0, P * b0 : P * b1], 0, P * b0, P * b1)
         for c in EARLY_TURNED:
             turn_res(c)
             sum_terms(c, res_t[c], True)
-        gather(early[:, 1, :], 1, 0, J)
+        for j0 in (0, HALF):
+            gather(early[:, 1, j0 : j0 + HALF], 1, j0, j0 + HALF)
+            interleave(x_all[:, PACK * j0 : PACK * (j0 + HALF)], early[:, :, j0 : j0 + HALF], slice(0, 2), False)
         sort_scales()
-        for c in range(chunks):
-            interleave(x_bf[c], early[:, :, cols(c)], slice(0, 2), False)
         gather(late[:, :J], 2, 0, J)
         for s in range(chunks + 5):
             if s < chunks:

@@ -104,7 +104,7 @@ def tile_list_hwaytanhP_kernel(
         load_res(4)
         nc.scalar.activation(warm_out[:], warm[:], ACT.Sigmoid)
 
-        heads_t = psum.tile([P, 2, HEADS, HEADS], F32, name="ke")
+        heads_t = psum.tile([P, 2, HEADS, HEADS], F32, name="ke", bufs=3)
         nc.tensor.transpose(heads_t[:].rearrange("j z g s -> j (z g s)"), wgt_rows[:], ident[:])
         for b0, b1 in SPREADS:
             heads = heads_t[:, 0, :, b0:b1].rearrange("j g s -> j s g")
@@ -112,7 +112,7 @@ def tile_list_hwaytanhP_kernel(
                 wgt_wide[:, b0:b1, :].rearrange("j s (g r) -> j s g r", r=GROUP),
                 heads.unsqueeze(3).to_broadcast([P, b1 - b0, HEADS, GROUP]),
             )
-            spread = psum.tile([P, b1 - b0, P], F32, name="ve")
+            spread = psum.tile([P, b1 - b0, P], F32, name="ve", bufs=3)
             for s in range(b0, b1):
                 nc.tensor.transpose(spread[:, s - b0, :], wgt_wide[:, s, :], ident[:])
             nc.scalar.copy(wgt_sb[:, P * b0 : P * b1], spread[:].rearrange("p s j -> p (s j)"))
@@ -192,7 +192,7 @@ def tile_list_hwaytanhP_kernel(
             if c in TURNED:
                 for b in range(w // P):
                     block = slice(P * b, P * (b + 1))
-                    ve = psum.tile([P, N], F32, name="ve")
+                    ve = psum.tile([P, N], F32, name="ve", bufs=3)
                     nc.tensor.matmul_mx(
                         ve[:], x_codes[c][:, block].bitcast(FP8X4), x_scales[c][:, block],
                         wv_raw[:].bitcast(FP8X4), scales_raw[V_ROW:, :], start=True, stop=True,
@@ -202,7 +202,7 @@ def tile_list_hwaytanhP_kernel(
                     )
             for rows in banks_of(c):
                 if c not in TURNED:
-                    ve = psum.tile([P, len(rows), w], F32, name="ve")
+                    ve = psum.tile([P, len(rows), w], F32, name="ve", bufs=3)
                     for i in rows:
                         nc.tensor.matmul_mx(
                             ve[:, i - rows[0], :], wv[:, i, :].bitcast(FP8X4), scales[V_ROW:, i, :],
@@ -210,7 +210,7 @@ def tile_list_hwaytanhP_kernel(
                         )
                     part = cand[c][:, w * rows[0] : w * (rows[-1] + 1)]
                     nc.scalar.activation(part, ve[:].rearrange("p i j -> p (i j)"), ACT.Tanh)
-                ke = psum.tile([P, len(rows), w], F32, name="ke")
+                ke = psum.tile([P, len(rows), w], F32, name="ke", bufs=3)
                 for i in rows:
                     nc.tensor.matmul_mx(
                         ke[:, i - rows[0], :], wk[:, i, :].bitcast(FP4X4), scales[:, i, :],

@@ -23,7 +23,7 @@ BANK = 512
 HEADS = 8
 HALF = J // 2
 WIDTHS = [128, 256, 256, 256, 128]
-X_ON_VECTOR = ()
+X_ON_VECTOR = (3,)
 Y_ON_VECTOR = (4,)
 EARLY_TURNED = ()
 LATE_TURNED = (3,)
@@ -108,7 +108,7 @@ def tile_list_hwaytanhP_kernel(
         nc.tensor.transpose(heads_t[:].rearrange("j z g s -> j (z g s)"), wgt_rows[:], ident[:])
         for b0, b1 in SPREADS:
             heads = heads_t[:, 0, :, b0:b1].rearrange("j g s -> j s g")
-            nc.scalar.copy(
+            nc.vector.tensor_copy(
                 wgt_wide[:, b0:b1, :].rearrange("j s (g r) -> j s g r", r=GROUP),
                 heads.unsqueeze(3).to_broadcast([P, b1 - b0, HEADS, GROUP]),
             )
@@ -221,7 +221,7 @@ def tile_list_hwaytanhP_kernel(
 
         def blend(c):
             w = WIDTHS[c]
-            halves = [slice(0, 2), slice(2, 4)]
+            halves = [slice(0, 2), slice(2, 4)] if c else [slice(0, PACK)]
             if c in TURNED:
                 gaps = [gap[c, n][:] for n in range(2)] if w > P else [gap[c, 0][:, h, :] for h in halves]
             else:

@@ -89,14 +89,14 @@ def tile_list_hwaytanhP_kernel(
         nc.sync.dma_start(wgt_rows[: P // 2, :], one_row.rearrange("g (s j) -> g s j", j=P))
         nc.sync.dma_start(offsets[:], offs)
         nc.sync.dma_start(planes[0][:], x_planes[:, 0, :])
-        load_scales(nc.sync, 0, wk_scales[0])
         nc.sync.dma_start(planes[1][:], x_planes[:, 1, :])
-        load_scales(nc.sync, V_ROW, wv_scales[0])
-        nc.sync.dma_start(bias[:], bg.rearrange("(p i) -> p i", i=PACK))
+        load_scales(nc.sync, 0, wk_scales[0])
+        load_scales(nc.gpsimd, V_ROW, wv_scales[0])
         nc.sync.dma_start(planes[2][:], x_planes[:, 2, :])
         nc.sync.dma_start(planes[3][:], x_planes[:, 3, :])
-        nc.sync.dma_start(wk_raw[:].bitcast(I32), wk_words[0].bitcast(I32))
         nc.sync.dma_start(wv_raw[:], wv_words[0].rearrange("p n i -> p (n i)").bitcast(I32))
+        nc.sync.dma_start(wk_raw[:].bitcast(I32), wk_words[0].bitcast(I32))
+        nc.sync.dma_start(bias[:], bg.rearrange("(p i) -> p i", i=PACK))
         load_res(0)
         load_res(1)
         load_res(2)
@@ -121,8 +121,8 @@ def tile_list_hwaytanhP_kernel(
             nc.vector.tensor_copy(scales[:], scales_raw[:].rearrange("p (m i) -> p i m", i=PACK))
 
         def sort_words():
-            nc.vector.tensor_copy(wk[:].bitcast(U16), wk_raw[:].bitcast(U16).rearrange("p (m i) -> p i m", i=PACK))
             nc.vector.tensor_copy(wv[:], wv_raw[:].rearrange("p (m i) -> p i m", i=PACK))
+            nc.vector.tensor_copy(wk[:].bitcast(U16), wk_raw[:].bitcast(U16).rearrange("p (m i) -> p i m", i=PACK))
 
         early = keep.tile([P, 2, J], F32, name="early")
         late = keep.tile([P, 2 * (J + SLOTS * SLOT)], F32, name="late")

@@ -23,10 +23,10 @@ BANK = 512
 HEADS = 8
 HALF = J // 2
 WIDTHS = [128, 256, 256, 256, 128]
-X_ON_VECTOR = (3,)
+X_ON_VECTOR = (3, 4)
 Y_ON_VECTOR = (4,)
 EARLY_TURNED = ()
-LATE_TURNED = (3,)
+LATE_TURNED = (3, 4)
 TURNED = EARLY_TURNED + LATE_TURNED
 SPREADS = [(0, 2), (5, 8), (2, 3), (3, 5)]
 SLOTS = 3
@@ -89,14 +89,14 @@ def tile_list_hwaytanhP_kernel(
         nc.sync.dma_start(wgt_rows[: P // 2, :], one_row.rearrange("g (s j) -> g s j", j=P))
         nc.sync.dma_start(offsets[:], offs)
         nc.sync.dma_start(planes[0][:], x_planes[:, 0, :])
-        nc.sync.dma_start(planes[1][:], x_planes[:, 1, :])
         load_scales(nc.sync, 0, wk_scales[0])
-        load_scales(nc.gpsimd, V_ROW, wv_scales[0])
+        nc.sync.dma_start(planes[1][:], x_planes[:, 1, :])
+        load_scales(nc.sync, V_ROW, wv_scales[0])
+        nc.sync.dma_start(bias[:], bg.rearrange("(p i) -> p i", i=PACK))
         nc.sync.dma_start(planes[2][:], x_planes[:, 2, :])
         nc.sync.dma_start(planes[3][:], x_planes[:, 3, :])
         nc.sync.dma_start(wv_raw[:], wv_words[0].rearrange("p n i -> p (n i)").bitcast(I32))
         nc.sync.dma_start(wk_raw[:].bitcast(I32), wk_words[0].bitcast(I32))
-        nc.sync.dma_start(bias[:], bg.rearrange("(p i) -> p i", i=PACK))
         load_res(0)
         load_res(1)
         load_res(2)
@@ -168,7 +168,7 @@ def tile_list_hwaytanhP_kernel(
 
         def turn_res(c):
             for b in range(WIDTHS[c] // P):
-                bank = psum.tile([P, PACK, P], F32, name="spare")
+                bank = psum.tile([P, PACK, P], F32, name="spare" if c < chunks - 1 else "ve", bufs=2 if c < chunks - 1 else 3)
                 for i in range(PACK):
                     nc.tensor.transpose(bank[:, i, :], res_sb[c][:, i, P * b : P * (b + 1)], ident[:])
                 nc.scalar.copy(by_block(res_t[c])[:, b, :, :], bank[:])
@@ -176,7 +176,7 @@ def tile_list_hwaytanhP_kernel(
         def sum_terms(c, src, first):
             for n, rows in enumerate(banks_of(c)):
                 if first:
-                    gap[c, n] = psum.tile([P, len(rows), WIDTHS[c]], F32, name="gap" if c in EARLY_TURNED else "spare")
+                    gap[c, n] = psum.tile([P, len(rows), WIDTHS[c]], F32, name="spare" if c < chunks - 1 else "ke", bufs=2 if c < chunks - 1 else 3)
                 terms = [(b, i) for b in range(WIDTHS[c] // P) for i in rows]
                 for m, (b, i) in enumerate(terms):
                     nc.tensor.matmul(
@@ -233,7 +233,10 @@ def tile_list_hwaytanhP_kernel(
                 nc.vector.tensor_tensor(step[c][:, h, :], src, gate[c][:, h, :], ALU.mult)
             for h in halves:
                 nc.vector.tensor_tensor(y[c][:, h, :], res_sb[c][:, h, :], step[c][:, h, :], ALU.subtract)
-            nc.sync.dma_start(out_rows[:, :, cols(c)], y[c][:])
+                if c in (3,):
+                    nc.sync.dma_start(out_rows[:, h, cols(c)], y[c][:, h, :])
+            if c not in (3,):
+                nc.sync.dma_start(out_rows[:, :, cols(c)], y[c][:])
 
         def round_y(c):
             interleave(y_bf[c][:], y[c][:], slice(0, PACK), c in Y_ON_VECTOR)

@@ -23,7 +23,7 @@ BANK = 512
 HEADS = 8
 HALF = J // 2
 WIDTHS = [128, 256, 256, 256, 128]
-X_ON_VECTOR = (3, 4)
+X_ON_VECTOR = (2, 3, 4)
 Y_ON_VECTOR = (4,)
 EARLY_TURNED = ()
 LATE_TURNED = (3, 4)
@@ -233,9 +233,9 @@ def tile_list_hwaytanhP_kernel(
                 nc.vector.tensor_tensor(step[c][:, h, :], src, gate[c][:, h, :], ALU.mult)
             for h in halves:
                 nc.vector.tensor_tensor(y[c][:, h, :], res_sb[c][:, h, :], step[c][:, h, :], ALU.subtract)
-                if c in (3,):
+                if c in (2, 3):
                     nc.sync.dma_start(out_rows[:, h, cols(c)], y[c][:, h, :])
-            if c not in (3,):
+            if c not in (2, 3):
                 nc.sync.dma_start(out_rows[:, :, cols(c)], y[c][:])
 
         def round_y(c):

@@ -19,20 +19,23 @@ ACT = mybir.ActivationFunctionType
 P = 128
 PACK = 4
 GROUP = 16
+HEADS = P // GROUP
 BANK = 512
-HEADS = 8
-HALF = J // 2
-WIDTHS = [128, 256, 256, 256, 128]
-X_ON_VECTOR = (2, 3, 4)
-Y_ON_VECTOR = (4,)
-EARLY_TURNED = ()
-LATE_TURNED = (3, 4)
-TURNED = EARLY_TURNED + LATE_TURNED
-SPREADS = [(0, 2), (5, 8), (2, 3), (3, 5)]
-SLOTS = 3
-SLOT = 256
+QUADRANT = 32
 V_ROW = 4
 RUN = 2
+
+WIDTHS = [128, 256, 256, 256, 128]
+LAST = len(WIDTHS) - 1
+TURNED = (LAST - 1, LAST)
+FRONTS = [(0,), (1,), (2,), (3, 4)]
+FRONTS_ON_SCALAR = 2
+SPREADS = [(0, 2), (5, 8), (2, 3), (3, 5)]
+STORED_BY_HALVES = (2, 3)
+BLEND_LAG = 3
+PLANES_LAG = 5
+PRODUCT_BANKS = 3
+TURN_BANKS = 2
 
 
 def tile_list_hwaytanhP_kernel(
@@ -49,7 +52,7 @@ def tile_list_hwaytanhP_kernel(
 
     with ExitStack() as ctx:
         keep = ctx.enter_context(tc.tile_pool(name="keep", bufs=1))
-        psum = ctx.enter_context(tc.psum_pool(name="psum", bufs=2))
+        psum = ctx.enter_context(tc.psum_pool(name="psum", bufs=PRODUCT_BANKS))
 
         offsets = keep.tile([P, J // GROUP], U16, name="offsets")
         wk_raw = keep.tile([P, 2 * N], U8, name="wk_raw", align_bytes=64)
@@ -77,34 +80,29 @@ def tile_list_hwaytanhP_kernel(
         def cols(c):
             return slice(starts[c], starts[c] + WIDTHS[c])
 
-        def load_scales(queue, first, rows):
-            for q in range(4):
-                dst = scales_raw[32 * q + first : 32 * q + first + 4, :]
-                queue.dma_start(dst.bitcast(I32), rows[4 * q : 4 * q + 4, :].bitcast(I32))
-
-        def load_res(c):
-            nc.sync.dma_start(res_sb[c][:], res_rows[:, :, cols(c)])
+        def load_scales(first, rows):
+            for q in range(P // QUADRANT):
+                dst = scales_raw[QUADRANT * q + first : QUADRANT * q + first + 4, :]
+                nc.sync.dma_start(dst.bitcast(I32), rows[4 * q : 4 * q + 4, :].bitcast(I32))
 
         one_row = wgt.rearrange("(g r) j -> g r j", r=GROUP)[:, 0, :]
         nc.sync.dma_start(wgt_rows[: P // 2, :], one_row.rearrange("g (s j) -> g s j", j=P))
         nc.sync.dma_start(offsets[:], offs)
         nc.sync.dma_start(planes[0][:], x_planes[:, 0, :])
-        load_scales(nc.sync, 0, wk_scales[0])
+        load_scales(0, wk_scales[0])
         nc.sync.dma_start(planes[1][:], x_planes[:, 1, :])
-        load_scales(nc.sync, V_ROW, wv_scales[0])
+        load_scales(V_ROW, wv_scales[0])
         nc.sync.dma_start(bias[:], bg.rearrange("(p i) -> p i", i=PACK))
         nc.sync.dma_start(planes[2][:], x_planes[:, 2, :])
         nc.sync.dma_start(planes[3][:], x_planes[:, 3, :])
-        nc.sync.dma_start(wv_raw[:], wv_words[0].rearrange("p n i -> p (n i)").bitcast(I32))
         nc.sync.dma_start(wk_raw[:].bitcast(I32), wk_words[0].bitcast(I32))
-        load_res(0)
-        load_res(1)
-        load_res(2)
-        load_res(3)
-        load_res(4)
+        nc.sync.dma_start(wv_raw[:], wv_words[0].rearrange("p n i -> p (n i)").bitcast(I32))
+        for c in range(chunks):
+            nc.sync.dma_start(res_sb[c][:], res_rows[:, :, cols(c)])
+
         nc.scalar.activation(warm_out[:], warm[:], ACT.Sigmoid)
 
-        heads_t = psum.tile([P, 2, HEADS, HEADS], F32, name="ke", bufs=3)
+        heads_t = psum.tile([P, 2, HEADS, J // P], F32, name="ke")
         nc.tensor.transpose(heads_t[:].rearrange("j z g s -> j (z g s)"), wgt_rows[:], ident[:])
         for b0, b1 in SPREADS:
             heads = heads_t[:, 0, :, b0:b1].rearrange("j g s -> j s g")
@@ -112,22 +110,14 @@ def tile_list_hwaytanhP_kernel(
                 wgt_wide[:, b0:b1, :].rearrange("j s (g r) -> j s g r", r=GROUP),
                 heads.unsqueeze(3).to_broadcast([P, b1 - b0, HEADS, GROUP]),
             )
-            spread = psum.tile([P, b1 - b0, P], F32, name="ve", bufs=3)
-            for s in range(b0, b1):
-                nc.tensor.transpose(spread[:, s - b0, :], wgt_wide[:, s, :], ident[:])
+            spread = psum.tile([P, b1 - b0, P], F32, name="ve")
+            for b in range(b0, b1):
+                nc.tensor.transpose(spread[:, b - b0, :], wgt_wide[:, b, :], ident[:])
             nc.scalar.copy(wgt_sb[:, P * b0 : P * b1], spread[:].rearrange("p s j -> p (s j)"))
 
-        def sort_scales():
-            nc.vector.tensor_copy(scales[:], scales_raw[:].rearrange("p (m i) -> p i m", i=PACK))
-
-        def sort_words():
-            nc.vector.tensor_copy(wv[:], wv_raw[:].rearrange("p (m i) -> p i m", i=PACK))
-            nc.vector.tensor_copy(wk[:].bitcast(U16), wk_raw[:].bitcast(U16).rearrange("p (m i) -> p i m", i=PACK))
-
         early = keep.tile([P, 2, J], F32, name="early")
-        late = keep.tile([P, 2 * (J + SLOTS * SLOT)], F32, name="late")
-        x_all = keep.tile([P, PACK * J], BF16, name="x_all", align_bytes=64)
-        x_bf = [x_all[:, PACK * starts[c] : PACK * (starts[c] + w)] for c, w in enumerate(WIDTHS)]
+        late = keep.tile([P, 2, J], F32, name="late")
+        x_bf = keep.tile([P, PACK * J], BF16, name="x_bf", align_bytes=64)
         x_codes = [keep.tile([P, w], I32, name="x_codes%d" % c, align_bytes=64) for c, w in enumerate(WIDTHS)]
         x_scales = [keep.tile([P, w], U8, name="x_scales%d" % c, align_bytes=64) for c, w in enumerate(WIDTHS)]
         cand = [keep.tile([P, PACK * w], F32, name="cand%d" % c) for c, w in enumerate(WIDTHS)]
@@ -147,52 +137,58 @@ def tile_list_hwaytanhP_kernel(
             per_bank = BANK // WIDTHS[c]
             return [range(i0, i0 + per_bank) for i0 in range(0, PACK, per_bank)]
 
+        def turn_bank(c, shape, free_tag):
+            if c == LAST:
+                return psum.tile(shape, F32, name=free_tag)
+            return psum.tile(shape, F32, name="turn", bufs=TURN_BANKS)
+
+        def sort_columns(dst, src):
+            nc.vector.tensor_copy(dst, src.rearrange("p (m i) -> p i m", i=PACK))
+
         def gather(dst, i, j0, j1):
             entries = offsets[:, j0 // GROUP : j1 // GROUP]
             nc.vector.tensor_tensor(dst, planes[i][:].indirect(entries), wgt_sb[:, j0:j1], ALU.mult)
 
-        def interleave(dst, src, rows, on_vector):
+        def interleave(copy, dst, src, rows):
             dst_view = dst.rearrange("p (u e i) -> p u i e", e=RUN, i=PACK)[:, :, rows, :]
-            src_view = src.rearrange("p i (u e) -> p u i e", e=RUN)
-            if on_vector:
-                nc.vector.tensor_copy(dst_view, src_view)
-            else:
-                nc.scalar.copy(dst_view, src_view)
+            copy(dst_view, src.rearrange("p i (u e) -> p u i e", e=RUN))
 
-        def front(c):
-            w = WIDTHS[c]
-            slot = J + SLOT * (c % SLOTS)
-            gather(late[:, slot : slot + w], 3, starts[c], starts[c] + w)
-            pair = late[:, starts[c] : 2 * slot - starts[c]].rearrange("p (r x) -> p r x", r=2)[:, :, :w]
-            interleave(x_bf[c], pair, slice(2, PACK), c in X_ON_VECTOR)
+        def last_planes(c):
+            for n, run in enumerate(FRONTS):
+                if run[0] == c:
+                    j0, j1 = starts[c], starts[run[-1]] + WIDTHS[run[-1]]
+                    gather(late[:, 1, j0:j1], 3, j0, j1)
+                    copy = nc.scalar.copy if n < FRONTS_ON_SCALAR else nc.vector.tensor_copy
+                    interleave(copy, x_bf[:, PACK * j0 : PACK * j1], late[:, :, j0:j1], slice(2, PACK))
 
         def turn_res(c):
             for b in range(WIDTHS[c] // P):
-                bank = psum.tile([P, PACK, P], F32, name="spare" if c < chunks - 1 else "ve", bufs=2 if c < chunks - 1 else 3)
+                bank = turn_bank(c, [P, PACK, P], "ve")
                 for i in range(PACK):
                     nc.tensor.transpose(bank[:, i, :], res_sb[c][:, i, P * b : P * (b + 1)], ident[:])
                 nc.scalar.copy(by_block(res_t[c])[:, b, :, :], bank[:])
 
-        def sum_terms(c, src, first):
+        def turn_back(c, src, opens):
             for n, rows in enumerate(banks_of(c)):
-                if first:
-                    gap[c, n] = psum.tile([P, len(rows), WIDTHS[c]], F32, name="spare" if c < chunks - 1 else "ke", bufs=2 if c < chunks - 1 else 3)
+                if opens:
+                    gap[c, n] = turn_bank(c, [P, len(rows), WIDTHS[c]], "ke")
                 terms = [(b, i) for b in range(WIDTHS[c] // P) for i in rows]
                 for m, (b, i) in enumerate(terms):
                     nc.tensor.matmul(
                         gap[c, n][:, i - rows[0], P * b : P * (b + 1)], by_block(src)[:, b, i, :], ident[:],
-                        start=(first and m == 0), stop=(not first and m == len(terms) - 1), is_transpose=True,
+                        start=(opens and m == 0), stop=(not opens and m == len(terms) - 1), is_transpose=True,
                     )
 
-        def quantise(c):
-            nc.vector.quantize_mx(x_codes[c][:].bitcast(FP8X4), x_scales[c][:], x_bf[c])
+        def quantise_x(c):
+            src = x_bf[:, PACK * starts[c] : PACK * (starts[c] + WIDTHS[c])]
+            nc.vector.quantize_mx(x_codes[c][:].bitcast(FP8X4), x_scales[c][:], src)
 
         def products(c):
             w = WIDTHS[c]
             if c in TURNED:
                 for b in range(w // P):
                     block = slice(P * b, P * (b + 1))
-                    ve = psum.tile([P, N], F32, name="ve", bufs=3)
+                    ve = psum.tile([P, N], F32, name="ve")
                     nc.tensor.matmul_mx(
                         ve[:], x_codes[c][:, block].bitcast(FP8X4), x_scales[c][:, block],
                         wv_raw[:].bitcast(FP8X4), scales_raw[V_ROW:, :], start=True, stop=True,
@@ -202,7 +198,7 @@ def tile_list_hwaytanhP_kernel(
                     )
             for rows in banks_of(c):
                 if c not in TURNED:
-                    ve = psum.tile([P, len(rows), w], F32, name="ve", bufs=3)
+                    ve = psum.tile([P, len(rows), w], F32, name="ve")
                     for i in rows:
                         nc.tensor.matmul_mx(
                             ve[:, i - rows[0], :], wv[:, i, :].bitcast(FP8X4), scales[V_ROW:, i, :],
@@ -210,7 +206,7 @@ def tile_list_hwaytanhP_kernel(
                         )
                     part = cand[c][:, w * rows[0] : w * (rows[-1] + 1)]
                     nc.scalar.activation(part, ve[:].rearrange("p i j -> p (i j)"), ACT.Tanh)
-                ke = psum.tile([P, len(rows), w], F32, name="ke", bufs=3)
+                ke = psum.tile([P, len(rows), w], F32, name="ke")
                 for i in rows:
                     nc.tensor.matmul_mx(
                         ke[:, i - rows[0], :], wk[:, i, :].bitcast(FP4X4), scales[:, i, :],
@@ -220,61 +216,61 @@ def tile_list_hwaytanhP_kernel(
                     nc.scalar.activation(gate[c][:, i, :], ke[:, i - rows[0], :], ACT.Sigmoid, bias=bias[:, i : i + 1])
 
         def blend(c):
-            w = WIDTHS[c]
-            halves = [slice(0, 2), slice(2, 4)] if c else [slice(0, PACK)]
-            if c in TURNED:
-                gaps = [gap[c, n][:] for n in range(2)] if w > P else [gap[c, 0][:, h, :] for h in halves]
+            halves = [slice(0, 2), slice(2, PACK)] if c > 0 else [slice(0, PACK)]
+            if c == LAST:
+                gaps = [gap[c, 0][:, h, :] for h in halves]
+            elif c in TURNED:
+                gaps = [gap[c, n][:] for n in range(len(halves))]
             else:
-                rows = cand[c][:].rearrange("p (i j) -> p i j", i=PACK)
+                tanh = cand[c][:].rearrange("p (i j) -> p i j", i=PACK)
                 for h in halves:
-                    nc.vector.tensor_tensor(diff[c][:, h, :], res_sb[c][:, h, :], rows[:, h, :], ALU.subtract)
+                    nc.vector.tensor_tensor(diff[c][:, h, :], res_sb[c][:, h, :], tanh[:, h, :], ALU.subtract)
                 gaps = [diff[c][:, h, :] for h in halves]
             for h, src in zip(halves, gaps):
                 nc.vector.tensor_tensor(step[c][:, h, :], src, gate[c][:, h, :], ALU.mult)
             for h in halves:
                 nc.vector.tensor_tensor(y[c][:, h, :], res_sb[c][:, h, :], step[c][:, h, :], ALU.subtract)
-                if c in (2, 3):
+                if c in STORED_BY_HALVES:
                     nc.sync.dma_start(out_rows[:, h, cols(c)], y[c][:, h, :])
-            if c not in (2, 3):
+            if c not in STORED_BY_HALVES:
                 nc.sync.dma_start(out_rows[:, :, cols(c)], y[c][:])
 
-        def round_y(c):
-            interleave(y_bf[c][:], y[c][:], slice(0, PACK), c in Y_ON_VECTOR)
-
         def hand_on(c):
+            copy = nc.vector.tensor_copy if c == LAST else nc.scalar.copy
+            interleave(copy, y_bf[c][:], y[c][:], slice(0, PACK))
             nc.vector.quantize_mx(y_codes[c][:].bitcast(FP8X4), y_scales[:, cols(c)], y_bf[c][:])
             nc.sync.dma_start(out_words[:, cols(c)], y_codes[c][:])
 
         for b0, b1 in SPREADS:
             gather(early[:, 0, P * b0 : P * b1], 0, P * b0, P * b1)
-        for c in EARLY_TURNED:
-            turn_res(c)
-            sum_terms(c, res_t[c], True)
-        for j0 in (0, HALF):
-            gather(early[:, 1, j0 : j0 + HALF], 1, j0, j0 + HALF)
-            interleave(x_all[:, PACK * j0 : PACK * (j0 + HALF)], early[:, :, j0 : j0 + HALF], slice(0, 2), False)
-        sort_scales()
-        gather(late[:, :J], 2, 0, J)
-        for s in range(chunks + 5):
-            if s < chunks:
-                front(s)
+        for j0, j1 in ((0, J // 2), (J // 2, J)):
+            gather(early[:, 1, j0:j1], 1, j0, j1)
+            interleave(nc.scalar.copy, x_bf[:, PACK * j0 : PACK * j1], early[:, :, j0:j1], slice(0, 2))
+        sort_columns(scales[:], scales_raw[:])
+        gather(late[:, 0, :], 2, 0, J)
+
+        for s in range(chunks + PLANES_LAG):
+            last_planes(s)
             if s == 1:
-                sort_words()
-            if 0 <= s - 1 < chunks:
-                quantise(s - 1)
-                if s - 1 in LATE_TURNED:
-                    turn_res(s - 1)
-                    sum_terms(s - 1, res_t[s - 1], True)
-                products(s - 1)
-                if s - 1 in TURNED:
-                    sum_terms(s - 1, cand[s - 1], False)
-            if 0 <= s - 3 < chunks:
-                blend(s - 3)
-            if 0 <= s - 5 < chunks:
-                round_y(s - 5)
-                hand_on(s - 5)
-        for q in range(4):
+                sort_columns(wk[:].bitcast(U16), wk_raw[:].bitcast(U16))
+                sort_columns(wv[:], wv_raw[:])
+            c = s - 1
+            if 0 <= c < chunks:
+                quantise_x(c)
+                if c in TURNED:
+                    turn_res(c)
+                    turn_back(c, res_t[c], True)
+                products(c)
+                if c in TURNED:
+                    turn_back(c, cand[c], False)
+            if 0 <= s - BLEND_LAG < chunks:
+                blend(s - BLEND_LAG)
+            if 0 <= s - PLANES_LAG < chunks:
+                hand_on(s - PLANES_LAG)
+
+        for q in range(P // QUADRANT):
             queue = nc.sync if q % 2 == 0 else nc.scalar
             queue.dma_start(
-                out_2[0][4 * q : 4 * q + 4, :].bitcast(I32), y_scales[32 * q : 32 * q + 4, :].bitcast(I32)
+                out_2[0][4 * q : 4 * q + 4, :].bitcast(I32),
+                y_scales[QUADRANT * q : QUADRANT * q + 4, :].bitcast(I32),
             )

@@ -87,8 +87,8 @@ def tile_list_hwaytanhP_kernel(
 
         one_row = wgt.rearrange("(g r) j -> g r j", r=GROUP)[:, 0, :]
         nc.sync.dma_start(wgt_rows[: P // 2, :], one_row.rearrange("g (s j) -> g s j", j=P))
-        nc.sync.dma_start(offsets[:], offs)
         nc.sync.dma_start(planes[0][:], x_planes[:, 0, :])
+        nc.sync.dma_start(offsets[:], offs)
         load_scales(0, wk_scales[0])
         nc.sync.dma_start(planes[1][:], x_planes[:, 1, :])
         load_scales(V_ROW, wv_scales[0])

@@ -31,7 +31,6 @@ TURNED = (LAST - 1, LAST)
 FRONTS = [(0,), (1,), (2,), (3, 4)]
 FRONTS_ON_SCALAR = 2
 SPREADS = [(0, 2), (5, 8), (2, 3), (3, 5)]
-STORED_BY_HALVES = (2, 3)
 BLEND_LAG = 3
 PLANES_LAG = 5
 PRODUCT_BANKS = 3
@@ -121,11 +120,14 @@ def tile_list_hwaytanhP_kernel(
         x_codes = [keep.tile([P, w], I32, name="x_codes%d" % c, align_bytes=64) for c, w in enumerate(WIDTHS)]
         x_scales = [keep.tile([P, w], U8, name="x_scales%d" % c, align_bytes=64) for c, w in enumerate(WIDTHS)]
         cand = [keep.tile([P, PACK * w], F32, name="cand%d" % c) for c, w in enumerate(WIDTHS)]
-        gate = [keep.tile([P, PACK, w], F32, name="gate%d" % c) for c, w in enumerate(WIDTHS)]
+        gate = [keep.tile([P, PACK, w], F32, name="gate%d" % c)[:] for c, w in enumerate(WIDTHS)]
+        joint = keep.tile([P, PACK + 2, WIDTHS[2]], F32, name="joint")
+        gate[3] = joint[:, 2:, :]
         diff = {c: keep.tile([P, PACK, w], F32, name="diff%d" % c) for c, w in enumerate(WIDTHS) if c not in TURNED}
         res_t = {c: keep.tile([P, PACK * WIDTHS[c]], F32, name="res_t%d" % c) for c in TURNED}
         step = [keep.tile([P, PACK, w], F32, name="step%d" % c) for c, w in enumerate(WIDTHS)]
-        y = [keep.tile([P, PACK, w], F32, name="y%d" % c) for c, w in enumerate(WIDTHS)]
+        y = [keep.tile([P, PACK, w], F32, name="y%d" % c)[:] for c, w in enumerate(WIDTHS)]
+        y[1] = cand[2][:].rearrange("p (i j) -> p i j", i=PACK)
         y_bf = [keep.tile([P, PACK * w], BF16, name="y_bf%d" % c, align_bytes=64) for c, w in enumerate(WIDTHS)]
         y_codes = [keep.tile([P, w], I32, name="y_codes%d" % c, align_bytes=64) for c, w in enumerate(WIDTHS)]
         gap = {}
@@ -215,29 +217,59 @@ def tile_list_hwaytanhP_kernel(
                 for i in rows:
                     nc.scalar.activation(gate[c][:, i, :], ke[:, i - rows[0], :], ACT.Sigmoid, bias=bias[:, i : i + 1])
 
-        def blend(c):
-            halves = [slice(0, 2), slice(2, PACK)] if c > 0 else [slice(0, PACK)]
+        def halves_of(c):
+            return [slice(0, 2), slice(2, PACK)] if c in TURNED else [slice(0, PACK)]
+
+        def subtract(c):
+            tanh = cand[c][:].rearrange("p (i j) -> p i j", i=PACK)
+            nc.vector.tensor_tensor(diff[c][:], res_sb[c][:], tanh, ALU.subtract)
+
+        def weigh(c, n):
+            h = halves_of(c)[n]
             if c == LAST:
-                gaps = [gap[c, 0][:, h, :] for h in halves]
+                src = gap[c, 0][:, h, :]
             elif c in TURNED:
-                gaps = [gap[c, n][:] for n in range(len(halves))]
+                src = gap[c, n][:]
             else:
-                tanh = cand[c][:].rearrange("p (i j) -> p i j", i=PACK)
-                for h in halves:
-                    nc.vector.tensor_tensor(diff[c][:, h, :], res_sb[c][:, h, :], tanh[:, h, :], ALU.subtract)
-                gaps = [diff[c][:, h, :] for h in halves]
-            for h, src in zip(halves, gaps):
-                nc.vector.tensor_tensor(step[c][:, h, :], src, gate[c][:, h, :], ALU.mult)
-            for h in halves:
-                nc.vector.tensor_tensor(y[c][:, h, :], res_sb[c][:, h, :], step[c][:, h, :], ALU.subtract)
-                if c in STORED_BY_HALVES:
-                    nc.sync.dma_start(out_rows[:, h, cols(c)], y[c][:, h, :])
-            if c not in STORED_BY_HALVES:
-                nc.sync.dma_start(out_rows[:, :, cols(c)], y[c][:])
+                src = diff[c][:]
+            nc.vector.tensor_tensor(step[c][:, h, :], src, gate[c][:, h, :], ALU.mult)
+
+        def take(c, n):
+            h = halves_of(max(c, LAST - 1) if c == 2 else c)[n]
+            nc.vector.tensor_tensor(y[c][:, h, :], res_sb[c][:, h, :], step[c][:, h, :], ALU.subtract)
+            if c != LAST:
+                nc.sync.dma_start(out_rows[:, h, cols(c)], y[c][:, h, :])
+            elif n == 1:
+                nc.sync.dma_start(out_rows[:, :, cols(c)], y[c])
+
+        def blend(c):
+            if c == 0:
+                subtract(0)
+                weigh(0, 0)
+                subtract(1)
+                take(0, 0)
+            if c == 1:
+                weigh(1, 0)
+                subtract(2)
+                take(1, 0)
+            if c == 2:
+                weigh(2, 0)
+                take(2, 0)
+                take(2, 1)
+            if c == 3:
+                weigh(3, 0)
+                weigh(3, 1)
+                take(3, 0)
+                take(3, 1)
+            if c == 4:
+                weigh(4, 0)
+                weigh(4, 1)
+                take(4, 0)
+                take(4, 1)
 
         def hand_on(c):
             copy = nc.vector.tensor_copy if c == LAST else nc.scalar.copy
-            interleave(copy, y_bf[c][:], y[c][:], slice(0, PACK))
+            interleave(copy, y_bf[c][:], y[c], slice(0, PACK))
             nc.vector.quantize_mx(y_codes[c][:].bitcast(FP8X4), y_scales[:, cols(c)], y_bf[c][:])
             nc.sync.dma_start(out_words[:, cols(c)], y_codes[c][:])
 

@@ -29,7 +29,7 @@ WIDTHS = [128, 256, 256, 256, 128]
 LAST = len(WIDTHS) - 1
 TURNED = (LAST - 1, LAST)
 FRONTS = [(0,), (1,), (2,), (3, 4)]
-FRONTS_ON_SCALAR = 2
+FRONTS_ON_SCALAR = 3
 SPREADS = [(0, 2), (5, 8), (2, 3), (3, 5)]
 BLEND_LAG = 3
 PLANES_LAG = 5
@@ -127,7 +127,6 @@ def tile_list_hwaytanhP_kernel(
         res_t = {c: keep.tile([P, PACK * WIDTHS[c]], F32, name="res_t%d" % c) for c in TURNED}
         step = [keep.tile([P, PACK, w], F32, name="step%d" % c) for c, w in enumerate(WIDTHS)]
         y = [keep.tile([P, PACK, w], F32, name="y%d" % c)[:] for c, w in enumerate(WIDTHS)]
-        y[1] = cand[2][:].rearrange("p (i j) -> p i j", i=PACK)
         y_bf = [keep.tile([P, PACK * w], BF16, name="y_bf%d" % c, align_bytes=64) for c, w in enumerate(WIDTHS)]
         y_codes = [keep.tile([P, w], I32, name="y_codes%d" % c, align_bytes=64) for c, w in enumerate(WIDTHS)]
         gap = {}
@@ -159,9 +158,13 @@ def tile_list_hwaytanhP_kernel(
             for n, run in enumerate(FRONTS):
                 if run[0] == c:
                     j0, j1 = starts[c], starts[run[-1]] + WIDTHS[run[-1]]
-                    gather(late[:, 1, j0:j1], 3, j0, j1)
+                    slot = late[:, :, j0:j1]
+                    if n == len(FRONTS) - 1:
+                        slot = late[:, :, : j1 - j0]
+                        gather(slot[:, 0, :], 2, j0, j1)
+                    gather(slot[:, 1, :], 3, j0, j1)
                     copy = nc.scalar.copy if n < FRONTS_ON_SCALAR else nc.vector.tensor_copy
-                    interleave(copy, x_bf[:, PACK * j0 : PACK * j1], late[:, :, j0:j1], slice(2, PACK))
+                    interleave(copy, x_bf[:, PACK * j0 : PACK * j1], slot, slice(2, PACK))
 
         def turn_res(c):
             for b in range(WIDTHS[c] // P):
@@ -279,7 +282,8 @@ def tile_list_hwaytanhP_kernel(
             gather(early[:, 1, j0:j1], 1, j0, j1)
             interleave(nc.scalar.copy, x_bf[:, PACK * j0 : PACK * j1], early[:, :, j0:j1], slice(0, 2))
         sort_columns(scales[:], scales_raw[:])
-        gather(late[:, 0, :], 2, 0, J)
+        held = starts[FRONTS[-1][0]]
+        gather(late[:, 0, :held], 2, 0, held)
 
         for s in range(chunks + PLANES_LAG):
             last_planes(s)

@@ -30,7 +30,8 @@ LAST = len(WIDTHS) - 1
 TURNED = (LAST - 1, LAST)
 FRONTS = [(0,), (1,), (2,), (3, 4)]
 FRONTS_ON_SCALAR = 3
-SPREADS = [(0, 2), (5, 8), (2, 3), (3, 5)]
+SPREADS = [(0, 1), (1, 3), (6, 8), (4, 6), (3, 4)]
+SPLIT = 448
 BLEND_LAG = 3
 PLANES_LAG = 5
 PRODUCT_BANKS = 3
@@ -278,7 +279,7 @@ def tile_list_hwaytanhP_kernel(
 
         for b0, b1 in SPREADS:
             gather(early[:, 0, P * b0 : P * b1], 0, P * b0, P * b1)
-        for j0, j1 in ((0, J // 2), (J // 2, J)):
+        for j0, j1 in ((0, SPLIT), (SPLIT, J)):
             gather(early[:, 1, j0:j1], 1, j0, j1)
             interleave(nc.scalar.copy, x_bf[:, PACK * j0 : PACK * j1], early[:, :, j0:j1], slice(0, 2))
         sort_columns(scales[:], scales_raw[:])

@@ -89,11 +89,11 @@ def tile_list_hwaytanhP_kernel(
         nc.sync.dma_start(wgt_rows[: P // 2, :], one_row.rearrange("g (s j) -> g s j", j=P))
         nc.sync.dma_start(planes[0][:], x_planes[:, 0, :])
         nc.sync.dma_start(offsets[:], offs)
-        load_scales(0, wk_scales[0])
         nc.sync.dma_start(planes[1][:], x_planes[:, 1, :])
+        load_scales(0, wk_scales[0])
+        nc.sync.dma_start(planes[2][:], x_planes[:, 2, :])
         load_scales(V_ROW, wv_scales[0])
         nc.sync.dma_start(bias[:], bg.rearrange("(p i) -> p i", i=PACK))
-        nc.sync.dma_start(planes[2][:], x_planes[:, 2, :])
         nc.sync.dma_start(planes[3][:], x_planes[:, 3, :])
         nc.sync.dma_start(wk_raw[:].bitcast(I32), wk_words[0].bitcast(I32))
         nc.sync.dma_start(wv_raw[:], wv_words[0].rearrange("p n i -> p (n i)").bitcast(I32))
@@ -282,9 +282,9 @@ def tile_list_hwaytanhP_kernel(
         for j0, j1 in ((0, SPLIT), (SPLIT, J)):
             gather(early[:, 1, j0:j1], 1, j0, j1)
             interleave(nc.scalar.copy, x_bf[:, PACK * j0 : PACK * j1], early[:, :, j0:j1], slice(0, 2))
-        sort_columns(scales[:], scales_raw[:])
         held = starts[FRONTS[-1][0]]
         gather(late[:, 0, :held], 2, 0, held)
+        sort_columns(scales[:], scales_raw[:])
 
         for s in range(chunks + PLANES_LAG):
             last_planes(s)

@@ -155,6 +155,8 @@ def tile_list_hwaytanhP_kernel(
             dst_view = dst.rearrange("p (u e i) -> p u i e", e=RUN, i=PACK)[:, :, rows, :]
             copy(dst_view, src.rearrange("p i (u e) -> p u i e", e=RUN))
 
+        tail = []
+
         def last_planes(c):
             for n, run in enumerate(FRONTS):
                 if run[0] == c:
@@ -165,7 +167,12 @@ def tile_list_hwaytanhP_kernel(
                         gather(slot[:, 0, :], 2, j0, j1)
                     gather(slot[:, 1, :], 3, j0, j1)
                     copy = nc.scalar.copy if n < FRONTS_ON_SCALAR else nc.vector.tensor_copy
-                    interleave(copy, x_bf[:, PACK * j0 : PACK * j1], slot, slice(2, PACK))
+                    if run[-1] == LAST:
+                        j1 = starts[LAST]
+                        tail.append(slot[:, :, j1 - j0 :])
+                    interleave(copy, x_bf[:, PACK * j0 : PACK * j1], slot[:, :, : j1 - j0], slice(2, PACK))
+            if c == LAST:
+                interleave(nc.scalar.copy, x_bf[:, PACK * starts[LAST] :], tail[0], slice(2, PACK))
 
         def turn_res(c):
             for b in range(WIDTHS[c] // P):

@@ -29,13 +29,16 @@ WIDTHS = [128, 256, 256, 256, 128]
 LAST = len(WIDTHS) - 1
 TURNED = (LAST - 1, LAST)
 FRONTS = [(0,), (1,), (2,), (3, 4)]
-FRONTS_ON_SCALAR = 3
+WOVEN_ON_VECTOR = 3
 SPREADS = [(0, 1), (1, 3), (6, 8), (4, 6), (3, 4)]
-SPLIT = 448
+SPLIT = P * SPREADS[-1][0] + P // 2
+FIRST_HALVED = 2
 BLEND_LAG = 3
 PLANES_LAG = 5
 PRODUCT_BANKS = 3
 TURN_BANKS = 2
+WHOLE = [slice(0, PACK)]
+HALVES = [slice(0, PACK // 2), slice(PACK // 2, PACK)]
 
 
 def tile_list_hwaytanhP_kernel(
@@ -121,13 +124,11 @@ def tile_list_hwaytanhP_kernel(
         x_codes = [keep.tile([P, w], I32, name="x_codes%d" % c, align_bytes=64) for c, w in enumerate(WIDTHS)]
         x_scales = [keep.tile([P, w], U8, name="x_scales%d" % c, align_bytes=64) for c, w in enumerate(WIDTHS)]
         cand = [keep.tile([P, PACK * w], F32, name="cand%d" % c) for c, w in enumerate(WIDTHS)]
-        gate = [keep.tile([P, PACK, w], F32, name="gate%d" % c)[:] for c, w in enumerate(WIDTHS)]
-        joint = keep.tile([P, PACK + 2, WIDTHS[2]], F32, name="joint")
-        gate[3] = joint[:, 2:, :]
+        gate = [keep.tile([P, PACK, w], F32, name="gate%d" % c) for c, w in enumerate(WIDTHS)]
         diff = {c: keep.tile([P, PACK, w], F32, name="diff%d" % c) for c, w in enumerate(WIDTHS) if c not in TURNED}
         res_t = {c: keep.tile([P, PACK * WIDTHS[c]], F32, name="res_t%d" % c) for c in TURNED}
         step = [keep.tile([P, PACK, w], F32, name="step%d" % c) for c, w in enumerate(WIDTHS)]
-        y = [keep.tile([P, PACK, w], F32, name="y%d" % c)[:] for c, w in enumerate(WIDTHS)]
+        y = [keep.tile([P, PACK, w], F32, name="y%d" % c) for c, w in enumerate(WIDTHS)]
         y_bf = [keep.tile([P, PACK * w], BF16, name="y_bf%d" % c, align_bytes=64) for c, w in enumerate(WIDTHS)]
         y_codes = [keep.tile([P, w], I32, name="y_codes%d" % c, align_bytes=64) for c, w in enumerate(WIDTHS)]
         gap = {}
@@ -155,24 +156,22 @@ def tile_list_hwaytanhP_kernel(
             dst_view = dst.rearrange("p (u e i) -> p u i e", e=RUN, i=PACK)[:, :, rows, :]
             copy(dst_view, src.rearrange("p i (u e) -> p u i e", e=RUN))
 
-        tail = []
+        held = starts[FRONTS[-1][0]]
+
+        def picked_late(j0, j1):
+            first = j0 - held if j0 >= held else j0
+            return late[:, :, first : first + j1 - j0]
 
         def last_planes(c):
-            for n, run in enumerate(FRONTS):
+            for run in FRONTS:
                 if run[0] == c:
-                    j0, j1 = starts[c], starts[run[-1]] + WIDTHS[run[-1]]
-                    slot = late[:, :, j0:j1]
-                    if n == len(FRONTS) - 1:
-                        slot = late[:, :, : j1 - j0]
-                        gather(slot[:, 0, :], 2, j0, j1)
-                    gather(slot[:, 1, :], 3, j0, j1)
-                    copy = nc.scalar.copy if n < FRONTS_ON_SCALAR else nc.vector.tensor_copy
-                    if run[-1] == LAST:
-                        j1 = starts[LAST]
-                        tail.append(slot[:, :, j1 - j0 :])
-                    interleave(copy, x_bf[:, PACK * j0 : PACK * j1], slot[:, :, : j1 - j0], slice(2, PACK))
-            if c == LAST:
-                interleave(nc.scalar.copy, x_bf[:, PACK * starts[LAST] :], tail[0], slice(2, PACK))
+                    j0, j1 = starts[c], cols(run[-1]).stop
+                    if j0 >= held:
+                        gather(picked_late(j0, j1)[:, 0, :], 2, j0, j1)
+                    gather(picked_late(j0, j1)[:, 1, :], 3, j0, j1)
+            j0, j1 = starts[c], cols(c).stop
+            copy = nc.vector.tensor_copy if c == WOVEN_ON_VECTOR else nc.scalar.copy
+            interleave(copy, x_bf[:, PACK * j0 : PACK * j1], picked_late(j0, j1), HALVES[1])
 
         def turn_res(c):
             for b in range(WIDTHS[c] // P):
@@ -228,59 +227,33 @@ def tile_list_hwaytanhP_kernel(
                 for i in rows:
                     nc.scalar.activation(gate[c][:, i, :], ke[:, i - rows[0], :], ACT.Sigmoid, bias=bias[:, i : i + 1])
 
-        def halves_of(c):
-            return [slice(0, 2), slice(2, PACK)] if c in TURNED else [slice(0, PACK)]
-
         def subtract(c):
             tanh = cand[c][:].rearrange("p (i j) -> p i j", i=PACK)
             nc.vector.tensor_tensor(diff[c][:], res_sb[c][:], tanh, ALU.subtract)
 
-        def weigh(c, n):
-            h = halves_of(c)[n]
-            if c == LAST:
-                src = gap[c, 0][:, h, :]
-            elif c in TURNED:
-                src = gap[c, n][:]
-            else:
-                src = diff[c][:]
-            nc.vector.tensor_tensor(step[c][:, h, :], src, gate[c][:, h, :], ALU.mult)
-
-        def take(c, n):
-            h = halves_of(max(c, LAST - 1) if c == 2 else c)[n]
-            nc.vector.tensor_tensor(y[c][:, h, :], res_sb[c][:, h, :], step[c][:, h, :], ALU.subtract)
-            if c != LAST:
-                nc.sync.dma_start(out_rows[:, h, cols(c)], y[c][:, h, :])
-            elif n == 1:
-                nc.sync.dma_start(out_rows[:, :, cols(c)], y[c])
-
         def blend(c):
             if c == 0:
-                subtract(0)
-                weigh(0, 0)
-                subtract(1)
-                take(0, 0)
-            if c == 1:
-                weigh(1, 0)
-                subtract(2)
-                take(1, 0)
-            if c == 2:
-                weigh(2, 0)
-                take(2, 0)
-                take(2, 1)
-            if c == 3:
-                weigh(3, 0)
-                weigh(3, 1)
-                take(3, 0)
-                take(3, 1)
-            if c == 4:
-                weigh(4, 0)
-                weigh(4, 1)
-                take(4, 0)
-                take(4, 1)
+                subtract(c)
+            if c == LAST:
+                gaps = [gap[c, 0][:, h, :] for h in HALVES]
+            elif c in TURNED:
+                gaps = [gap[c, n][:] for n in range(len(HALVES))]
+            else:
+                gaps = [diff[c][:]]
+            for h, src in zip(HALVES if c in TURNED else WHOLE, gaps):
+                nc.vector.tensor_tensor(step[c][:, h, :], src, gate[c][:, h, :], ALU.mult)
+            if c + 1 < TURNED[0]:
+                subtract(c + 1)
+            for h in HALVES if c >= FIRST_HALVED else WHOLE:
+                nc.vector.tensor_tensor(y[c][:, h, :], res_sb[c][:, h, :], step[c][:, h, :], ALU.subtract)
+                if c < LAST:
+                    nc.sync.dma_start(out_rows[:, h, cols(c)], y[c][:, h, :])
+            if c == LAST:
+                nc.sync.dma_start(out_rows[:, :, cols(c)], y[c][:])
 
         def hand_on(c):
             copy = nc.vector.tensor_copy if c == LAST else nc.scalar.copy
-            interleave(copy, y_bf[c][:], y[c], slice(0, PACK))
+            interleave(copy, y_bf[c][:], y[c][:], WHOLE[0])
             nc.vector.quantize_mx(y_codes[c][:].bitcast(FP8X4), y_scales[:, cols(c)], y_bf[c][:])
             nc.sync.dma_start(out_words[:, cols(c)], y_codes[c][:])
 
@@ -288,13 +261,13 @@ def tile_list_hwaytanhP_kernel(
             gather(early[:, 0, P * b0 : P * b1], 0, P * b0, P * b1)
         for j0, j1 in ((0, SPLIT), (SPLIT, J)):
             gather(early[:, 1, j0:j1], 1, j0, j1)
-            interleave(nc.scalar.copy, x_bf[:, PACK * j0 : PACK * j1], early[:, :, j0:j1], slice(0, 2))
-        held = starts[FRONTS[-1][0]]
+            interleave(nc.scalar.copy, x_bf[:, PACK * j0 : PACK * j1], early[:, :, j0:j1], HALVES[0])
         gather(late[:, 0, :held], 2, 0, held)
         sort_columns(scales[:], scales_raw[:])
 
         for s in range(chunks + PLANES_LAG):
-            last_planes(s)
+            if s < chunks:
+                last_planes(s)
             if s == 1:
                 sort_columns(wk[:].bitcast(U16), wk_raw[:].bitcast(U16))
                 sort_columns(wv[:], wv_raw[:])

@@ -88,8 +88,8 @@ def tile_list_hwaytanhP_kernel(
                 dst = scales_raw[QUADRANT * q + first : QUADRANT * q + first + 4, :]
                 nc.sync.dma_start(dst.bitcast(I32), rows[4 * q : 4 * q + 4, :].bitcast(I32))
 
-        one_row = wgt.rearrange("(g r) j -> g r j", r=GROUP)[:, 0, :]
-        nc.sync.dma_start(wgt_rows[: P // 2, :], one_row.rearrange("g (s j) -> g s j", j=P))
+        half_rows = wgt.rearrange("p (h j) -> (p h) j", h=2)[:: GROUP + 1, :]
+        nc.sync.dma_start(wgt_rows[: P // 2, :], half_rows.rearrange("q (s j) -> q s j", j=P))
         nc.sync.dma_start(planes[0][:], x_planes[:, 0, :])
         nc.sync.dma_start(offsets[:], offs)
         nc.sync.dma_start(planes[1][:], x_planes[:, 1, :])
@@ -145,8 +145,10 @@ def tile_list_hwaytanhP_kernel(
                 return psum.tile(shape, F32, name=free_tag)
             return psum.tile(shape, F32, name="turn", bufs=TURN_BANKS)
 
-        def sort_columns(dst, src):
-            nc.vector.tensor_copy(dst, src.rearrange("p (m i) -> p i m", i=PACK))
+        def sort_columns(dst, src, run):
+            nc.vector.tensor_copy(
+                dst.rearrange("p i (u e) -> p u i e", e=run), src.rearrange("p (u e i) -> p u i e", e=run, i=PACK)
+            )
 
         def gather(dst, i, j0, j1):
             entries = offsets[:, j0 // GROUP : j1 // GROUP]
@@ -263,14 +265,14 @@ def tile_list_hwaytanhP_kernel(
             gather(early[:, 1, j0:j1], 1, j0, j1)
             interleave(nc.scalar.copy, x_bf[:, PACK * j0 : PACK * j1], early[:, :, j0:j1], HALVES[0])
         gather(late[:, 0, :held], 2, 0, held)
-        sort_columns(scales[:], scales_raw[:])
+        sort_columns(scales[:], scales_raw[:], 16)
 
         for s in range(chunks + PLANES_LAG):
             if s < chunks:
                 last_planes(s)
             if s == 1:
-                sort_columns(wk[:].bitcast(U16), wk_raw[:].bitcast(U16))
-                sort_columns(wv[:], wv_raw[:])
+                sort_columns(wk[:].bitcast(U16), wk_raw[:].bitcast(U16), 8)
+                sort_columns(wv[:], wv_raw[:], 4)
             c = s - 1
             if 0 <= c < chunks:
                 quantise_x(c)

@@ -288,8 +288,7 @@ def tile_list_hwaytanhP_kernel(
                 hand_on(s - PLANES_LAG)
 
         for q in range(P // QUADRANT):
-            queue = nc.sync if q % 2 == 0 else nc.scalar
-            queue.dma_start(
+            nc.sync.dma_start(
                 out_2[0][4 * q : 4 * q + 4, :].bitcast(I32),
                 y_scales[QUADRANT * q : QUADRANT * q + 4, :].bitcast(I32),
             )

@@ -130,7 +130,7 @@ def tile_list_hwaytanhP_kernel(
         step = [keep.tile([P, PACK, w], F32, name="step%d" % c) for c, w in enumerate(WIDTHS)]
         y = [keep.tile([P, PACK, w], F32, name="y%d" % c) for c, w in enumerate(WIDTHS)]
         y_bf = [keep.tile([P, PACK * w], BF16, name="y_bf%d" % c, align_bytes=64) for c, w in enumerate(WIDTHS)]
-        y_codes = [keep.tile([P, w], I32, name="y_codes%d" % c, align_bytes=64) for c, w in enumerate(WIDTHS)]
+        y_codes = keep.tile([P, J], I32, name="y_codes", align_bytes=64)
         gap = {}
 
         def by_block(tile):
@@ -256,8 +256,10 @@ def tile_list_hwaytanhP_kernel(
         def hand_on(c):
             copy = nc.vector.tensor_copy if c == LAST else nc.scalar.copy
             interleave(copy, y_bf[c][:], y[c][:], WHOLE[0])
-            nc.vector.quantize_mx(y_codes[c][:].bitcast(FP8X4), y_scales[:, cols(c)], y_bf[c][:])
-            nc.sync.dma_start(out_words[:, cols(c)], y_codes[c][:])
+            nc.vector.quantize_mx(y_codes[:, cols(c)].bitcast(FP8X4), y_scales[:, cols(c)], y_bf[c][:])
+            if c != LAST - 1:
+                span = slice(starts[c - 1] if c == LAST else starts[c], cols(c).stop)
+                nc.sync.dma_start(out_words[:, span], y_codes[:, span])
 
         for b0, b1 in SPREADS:
             gather(early[:, 0, P * b0 : P * b1], 0, P * b0, P * b1)
@@ -287,8 +289,5 @@ def tile_list_hwaytanhP_kernel(
             if 0 <= s - PLANES_LAG < chunks:
                 hand_on(s - PLANES_LAG)
 
-        for q in range(P // QUADRANT):
-            nc.sync.dma_start(
-                out_2[0][4 * q : 4 * q + 4, :].bitcast(I32),
-                y_scales[QUADRANT * q : QUADRANT * q + 4, :].bitcast(I32),
-            )
+        for r in range(4):
+            nc.sync.dma_start(out_2[0][r::4, :].bitcast(I32), y_scales[r::QUADRANT, :].bitcast(I32))

@@ -248,10 +248,7 @@ def tile_list_hwaytanhP_kernel(
                 subtract(c + 1)
             for h in HALVES if c >= FIRST_HALVED else WHOLE:
                 nc.vector.tensor_tensor(y[c][:, h, :], res_sb[c][:, h, :], step[c][:, h, :], ALU.subtract)
-                if c < LAST:
-                    nc.sync.dma_start(out_rows[:, h, cols(c)], y[c][:, h, :])
-            if c == LAST:
-                nc.sync.dma_start(out_rows[:, :, cols(c)], y[c][:])
+                nc.sync.dma_start(out_rows[:, h, cols(c)], y[c][:, h, :])
 
         def hand_on(c):
             copy = nc.vector.tensor_copy if c == LAST else nc.scalar.copy
@@ -289,5 +286,8 @@ def tile_list_hwaytanhP_kernel(
             if 0 <= s - PLANES_LAG < chunks:
                 hand_on(s - PLANES_LAG)
 
-        for r in range(4):
-            nc.sync.dma_start(out_2[0][r::4, :].bitcast(I32), y_scales[r::QUADRANT, :].bitcast(I32))
+        for q in range(P // QUADRANT):
+            nc.sync.dma_start(
+                out_2[0][4 * q : 4 * q + 4, :].bitcast(I32),
+                y_scales[QUADRANT * q : QUADRANT * q + 4, :].bitcast(I32),
+            )

from contextlib import ExitStack

import concourse.mybir as mybir
from concourse.masks import make_identity

K, N, T, J = 512, 512, 2048, 1024
FLOPS = 2 * 2 * K * N * J

F32 = mybir.dt.float32
BF16 = mybir.dt.bfloat16
I32 = mybir.dt.int32
U16 = mybir.dt.uint16
U8 = mybir.dt.uint8
FP8X4 = mybir.dt.float8_e4m3fn_x4
FP4X4 = mybir.dt.float4_e2m1fn_x4
ALU = mybir.AluOpType
ACT = mybir.ActivationFunctionType

P = 128
PACK = 4
GROUP = 16
HEADS = P // GROUP
BANK = 512
QUADRANT = 32
V_ROW = 4
RUN = 2

WIDTHS = [128, 256, 256, 256, 128]
LAST = len(WIDTHS) - 1
TURNED = (LAST - 1, LAST)
FRONTS = [(0,), (1,), (2,), (3, 4)]
WOVEN_ON_VECTOR = 3
SPREADS = [(0, 1), (1, 3), (6, 8), (4, 6), (3, 4)]
SPLIT = P * SPREADS[-1][0] + P // 2
FIRST_HALVED = 2
BLEND_LAG = 3
PLANES_LAG = 5
PRODUCT_BANKS = 3
TURN_BANKS = 2
WHOLE = [slice(0, PACK)]
HALVES = [slice(0, PACK // 2), slice(PACK // 2, PACK)]


def tile_list_hwaytanhP_kernel(
    tc, xT, wgt, wk_words, wk_scales, wv_words, wv_scales, bg, res, offs, out_0, out_1, out_2
):
    nc = tc.nc
    starts = [sum(WIDTHS[:c]) for c in range(len(WIDTHS))]
    chunks = len(WIDTHS)

    x_planes = xT.rearrange("(p i) t -> p i t", i=PACK)
    res_rows = res.rearrange("(p i) j -> p i j", i=PACK)
    out_rows = out_0.rearrange("(p i) j -> p i j", i=PACK)
    out_words = out_1[0].rearrange("p j i -> p (j i)").bitcast(I32)

    with ExitStack() as ctx:
        keep = ctx.enter_context(tc.tile_pool(name="keep", bufs=1))
        psum = ctx.enter_context(tc.psum_pool(name="psum", bufs=PRODUCT_BANKS))

        offsets = keep.tile([P, J // GROUP], U16, name="offsets")
        wk_raw = keep.tile([P, 2 * N], U8, name="wk_raw", align_bytes=64)
        wv_raw = keep.tile([P, N], I32, name="wv_raw", align_bytes=64)
        scales_raw = keep.tile([P, N], U8, name="scales_raw", align_bytes=64)
        wk = keep.tile([P, PACK, 2 * P], U8, name="wk", align_bytes=64)
        wv = keep.tile([P, PACK, P], I32, name="wv", align_bytes=64)
        scales = keep.tile([P, PACK, P], U8, name="scales", align_bytes=64)
        bias = keep.tile([P, PACK], F32, name="bias")
        warm = keep.tile([P, 8], F32, name="warm")
        warm_out = keep.tile([P, 8], F32, name="warm_out")
        planes = [keep.tile([P, T], F32, name="plane%d" % i) for i in range(PACK)]
        wgt_sb = keep.tile([P, J], F32, name="wgt_sb")
        res_sb = [keep.tile([P, PACK, w], F32, name="res%d" % c) for c, w in enumerate(WIDTHS)]
        y_scales = keep.tile([P, J], U8, name="y_scales", align_bytes=64)
        wgt_rows = keep.tile([P, P], F32, name="wgt_rows")
        wgt_wide = keep.tile([P, HEADS, P], F32, name="wgt_wide")
        ident = keep.tile([P, P], F32, name="ident")

        nc.vector.memset(scales_raw[:].bitcast(I32), 0)
        nc.vector.memset(warm[:], 0.0)
        nc.vector.memset(wgt_rows[P // 2 :, :], 0.0)
        make_identity(nc, ident[:])

        def cols(c):
            return slice(starts[c], starts[c] + WIDTHS[c])

        def load_scales(first, rows):
            for q in range(P // QUADRANT):
                dst = scales_raw[QUADRANT * q + first : QUADRANT * q + first + 4, :]
                nc.sync.dma_start(dst.bitcast(I32), rows[4 * q : 4 * q + 4, :].bitcast(I32))

        half_rows = wgt.rearrange("p (h j) -> (p h) j", h=2)[:: GROUP + 1, :]
        nc.sync.dma_start(wgt_rows[: P // 2, :], half_rows.rearrange("q (s j) -> q s j", j=P))
        nc.sync.dma_start(planes[0][:], x_planes[:, 0, :])
        nc.sync.dma_start(offsets[:], offs)
        nc.sync.dma_start(planes[1][:], x_planes[:, 1, :])
        load_scales(0, wk_scales[0])
        nc.sync.dma_start(planes[2][:], x_planes[:, 2, :])
        load_scales(V_ROW, wv_scales[0])
        nc.sync.dma_start(bias[:], bg.rearrange("(p i) -> p i", i=PACK))
        nc.sync.dma_start(planes[3][:], x_planes[:, 3, :])
        nc.sync.dma_start(wk_raw[:].bitcast(I32), wk_words[0].bitcast(I32))
        nc.sync.dma_start(wv_raw[:], wv_words[0].rearrange("p n i -> p (n i)").bitcast(I32))
        for c in range(chunks):
            nc.sync.dma_start(res_sb[c][:], res_rows[:, :, cols(c)])

        nc.scalar.activation(warm_out[:], warm[:], ACT.Sigmoid)

        heads_t = psum.tile([P, 2, HEADS, J // P], F32, name="ke")
        nc.tensor.transpose(heads_t[:].rearrange("j z g s -> j (z g s)"), wgt_rows[:], ident[:])
        for b0, b1 in SPREADS:
            heads = heads_t[:, 0, :, b0:b1].rearrange("j g s -> j s g")
            nc.vector.tensor_copy(
                wgt_wide[:, b0:b1, :].rearrange("j s (g r) -> j s g r", r=GROUP),
                heads.unsqueeze(3).to_broadcast([P, b1 - b0, HEADS, GROUP]),
            )
            spread = psum.tile([P, b1 - b0, P], F32, name="ve")
            for b in range(b0, b1):
                nc.tensor.transpose(spread[:, b - b0, :], wgt_wide[:, b, :], ident[:])
            nc.scalar.copy(wgt_sb[:, P * b0 : P * b1], spread[:].rearrange("p s j -> p (s j)"))

        early = keep.tile([P, 2, J], F32, name="early")
        late = keep.tile([P, 2, J], F32, name="late")
        x_bf = keep.tile([P, PACK * J], BF16, name="x_bf", align_bytes=64)
        x_codes = [keep.tile([P, w], I32, name="x_codes%d" % c, align_bytes=64) for c, w in enumerate(WIDTHS)]
        x_scales = [keep.tile([P, w], U8, name="x_scales%d" % c, align_bytes=64) for c, w in enumerate(WIDTHS)]
        cand = [keep.tile([P, PACK * w], F32, name="cand%d" % c) for c, w in enumerate(WIDTHS)]
        gate = [keep.tile([P, PACK, w], F32, name="gate%d" % c) for c, w in enumerate(WIDTHS)]
        diff = {c: keep.tile([P, PACK, w], F32, name="diff%d" % c) for c, w in enumerate(WIDTHS) if c not in TURNED}
        res_t = {c: keep.tile([P, PACK * WIDTHS[c]], F32, name="res_t%d" % c) for c in TURNED}
        step = [keep.tile([P, PACK, w], F32, name="step%d" % c) for c, w in enumerate(WIDTHS)]
        y = [keep.tile([P, PACK, w], F32, name="y%d" % c) for c, w in enumerate(WIDTHS)]
        y_bf = [keep.tile([P, PACK * w], BF16, name="y_bf%d" % c, align_bytes=64) for c, w in enumerate(WIDTHS)]
        y_codes = keep.tile([P, J], I32, name="y_codes", align_bytes=64)
        gap = {}

        def by_block(tile):
            return tile[:].rearrange("j (b i m) -> j b i m", i=PACK, m=P)

        def banks_of(c):
            per_bank = BANK // WIDTHS[c]
            return [range(i0, i0 + per_bank) for i0 in range(0, PACK, per_bank)]

        def turn_bank(c, shape, free_tag):
            if c == LAST:
                return psum.tile(shape, F32, name=free_tag)
            return psum.tile(shape, F32, name="turn", bufs=TURN_BANKS)

        def sort_columns(dst, src, run):
            nc.vector.tensor_copy(
                dst.rearrange("p i (u e) -> p u i e", e=run), src.rearrange("p (u e i) -> p u i e", e=run, i=PACK)
            )

        def gather(dst, i, j0, j1):
            entries = offsets[:, j0 // GROUP : j1 // GROUP]
            nc.vector.tensor_tensor(dst, planes[i][:].indirect(entries), wgt_sb[:, j0:j1], ALU.mult)

        def interleave(copy, dst, src, rows):
            dst_view = dst.rearrange("p (u e i) -> p u i e", e=RUN, i=PACK)[:, :, rows, :]
            copy(dst_view, src.rearrange("p i (u e) -> p u i e", e=RUN))

        held = starts[FRONTS[-1][0]]

        def picked_late(j0, j1):
            first = j0 - held if j0 >= held else j0
            return late[:, :, first : first + j1 - j0]

        def last_planes(c):
            for run in FRONTS:
                if run[0] == c:
                    j0, j1 = starts[c], cols(run[-1]).stop
                    if j0 >= held:
                        gather(picked_late(j0, j1)[:, 0, :], 2, j0, j1)
                    gather(picked_late(j0, j1)[:, 1, :], 3, j0, j1)
            j0, j1 = starts[c], cols(c).stop
            copy = nc.vector.tensor_copy if c == WOVEN_ON_VECTOR else nc.scalar.copy
            interleave(copy, x_bf[:, PACK * j0 : PACK * j1], picked_late(j0, j1), HALVES[1])

        def turn_res(c):
            for b in range(WIDTHS[c] // P):
                bank = turn_bank(c, [P, PACK, P], "ve")
                for i in range(PACK):
                    nc.tensor.transpose(bank[:, i, :], res_sb[c][:, i, P * b : P * (b + 1)], ident[:])
                nc.scalar.copy(by_block(res_t[c])[:, b, :, :], bank[:])

        def turn_back(c, src, opens):
            for n, rows in enumerate(banks_of(c)):
                if opens:
                    gap[c, n] = turn_bank(c, [P, len(rows), WIDTHS[c]], "ke")
                terms = [(b, i) for b in range(WIDTHS[c] // P) for i in rows]
                for m, (b, i) in enumerate(terms):
                    nc.tensor.matmul(
                        gap[c, n][:, i - rows[0], P * b : P * (b + 1)], by_block(src)[:, b, i, :], ident[:],
                        start=(opens and m == 0), stop=(not opens and m == len(terms) - 1), is_transpose=True,
                    )

        def quantise_x(c):
            src = x_bf[:, PACK * starts[c] : PACK * (starts[c] + WIDTHS[c])]
            nc.vector.quantize_mx(x_codes[c][:].bitcast(FP8X4), x_scales[c][:], src)

        def products(c):
            w = WIDTHS[c]
            if c in TURNED:
                for b in range(w // P):
                    block = slice(P * b, P * (b + 1))
                    ve = psum.tile([P, N], F32, name="ve")
                    nc.tensor.matmul_mx(
                        ve[:], x_codes[c][:, block].bitcast(FP8X4), x_scales[c][:, block],
                        wv_raw[:].bitcast(FP8X4), scales_raw[V_ROW:, :], start=True, stop=True,
                    )
                    nc.scalar.activation(
                        by_block(cand[c])[:, b, :, :], ve[:].rearrange("j (m i) -> j i m", i=PACK), ACT.Tanh, scale=-1.0
                    )
            for rows in banks_of(c):
                if c not in TURNED:
                    ve = psum.tile([P, len(rows), w], F32, name="ve")
                    for i in rows:
                        nc.tensor.matmul_mx(
                            ve[:, i - rows[0], :], wv[:, i, :].bitcast(FP8X4), scales[V_ROW:, i, :],
                            x_codes[c][:].bitcast(FP8X4), x_scales[c][:], start=True, stop=True,
                        )
                    part = cand[c][:, w * rows[0] : w * (rows[-1] + 1)]
                    nc.scalar.activation(part, ve[:].rearrange("p i j -> p (i j)"), ACT.Tanh)
                ke = psum.tile([P, len(rows), w], F32, name="ke")
                for i in rows:
                    nc.tensor.matmul_mx(
                        ke[:, i - rows[0], :], wk[:, i, :].bitcast(FP4X4), scales[:, i, :],
                        x_codes[c][:].bitcast(FP8X4), x_scales[c][:], start=True, stop=True,
                    )
                for i in rows:
                    nc.scalar.activation(gate[c][:, i, :], ke[:, i - rows[0], :], ACT.Sigmoid, bias=bias[:, i : i + 1])

        def subtract(c):
            tanh = cand[c][:].rearrange("p (i j) -> p i j", i=PACK)
            nc.vector.tensor_tensor(diff[c][:], res_sb[c][:], tanh, ALU.subtract)

        def blend(c):
            if c == 0:
                subtract(c)
            if c == LAST:
                gaps = [gap[c, 0][:, h, :] for h in HALVES]
            elif c in TURNED:
                gaps = [gap[c, n][:] for n in range(len(HALVES))]
            else:
                gaps = [diff[c][:]]
            for h, src in zip(HALVES if c in TURNED else WHOLE, gaps):
                nc.vector.tensor_tensor(step[c][:, h, :], src, gate[c][:, h, :], ALU.mult)
            if c + 1 < TURNED[0]:
                subtract(c + 1)
            for h in HALVES if c >= FIRST_HALVED else WHOLE:
                nc.vector.tensor_tensor(y[c][:, h, :], res_sb[c][:, h, :], step[c][:, h, :], ALU.subtract)
                nc.sync.dma_start(out_rows[:, h, cols(c)], y[c][:, h, :])

        def hand_on(c):
            copy = nc.vector.tensor_copy if c == LAST else nc.scalar.copy
            interleave(copy, y_bf[c][:], y[c][:], WHOLE[0])
            nc.vector.quantize_mx(y_codes[:, cols(c)].bitcast(FP8X4), y_scales[:, cols(c)], y_bf[c][:])
            if c != LAST - 1:
                span = slice(starts[c - 1] if c == LAST else starts[c], cols(c).stop)
                nc.sync.dma_start(out_words[:, span], y_codes[:, span])

        for b0, b1 in SPREADS:
            gather(early[:, 0, P * b0 : P * b1], 0, P * b0, P * b1)
        for j0, j1 in ((0, SPLIT), (SPLIT, J)):
            gather(early[:, 1, j0:j1], 1, j0, j1)
            interleave(nc.scalar.copy, x_bf[:, PACK * j0 : PACK * j1], early[:, :, j0:j1], HALVES[0])
        gather(late[:, 0, :held], 2, 0, held)
        sort_columns(scales[:], scales_raw[:], 16)

        for s in range(chunks + PLANES_LAG):
            if s < chunks:
                last_planes(s)
            if s == 1:
                sort_columns(wk[:].bitcast(U16), wk_raw[:].bitcast(U16), 8)
                sort_columns(wv[:], wv_raw[:], 4)
            c = s - 1
            if 0 <= c < chunks:
                quantise_x(c)
                if c in TURNED:
                    turn_res(c)
                    turn_back(c, res_t[c], True)
                products(c)
                if c in TURNED:
                    turn_back(c, cand[c], False)
            if 0 <= s - BLEND_LAG < chunks:
                blend(s - BLEND_LAG)
            if 0 <= s - PLANES_LAG < chunks:
                hand_on(s - PLANES_LAG)

        for q in range(P // QUADRANT):
            nc.sync.dma_start(
                out_2[0][4 * q : 4 * q + 4, :].bitcast(I32),
                y_scales[QUADRANT * q : QUADRANT * q + 4, :].bitcast(I32),
            )
